import numpy as np
import ml_dtypes


def mxq(x, axis, fmt="e4m3"):
    dtype, down = {"e4m3": (ml_dtypes.float8_e4m3fn, 7), "e5m2": (ml_dtypes.float8_e5m2, 14)}[fmt]
    v = np.moveaxis(np.asarray(x, np.float32).astype(ml_dtypes.bfloat16).astype(np.float64), axis, -1)
    blocks = v.reshape(v.shape[:-1] + (-1, 32))
    amax = np.abs(blocks).max(-1, keepdims=True)
    byte = np.maximum(np.where(amax > 0, np.frexp(amax)[1] - 1 + 127, 0) - down, 1)
    scale = np.exp2(byte - 127.0)
    codes = (blocks / scale).astype(np.float32).astype(dtype).astype(np.float64)
    return np.moveaxis((codes * scale).reshape(v.shape), -1, axis)


WIDE = False


def mx_kscale(k):
    if not WIDE:
        return np.ones(k)
    levels = np.array([10, -10, 5, -5, 0])
    if k % 512:
        return np.exp2(np.random.permutation(np.resize(levels, k // 32))).repeat(32)
    a = np.empty((k // 512, 16))
    for p in range(k // 512):
        a[p, :8] = np.random.permutation(np.resize(levels, 8))
        for g in range(8):
            far = levels[np.abs(levels - a[p, g]) >= 10]
            a[p, g + 8] = far[np.random.randint(len(far))]
    return np.exp2(a.ravel()).repeat(32)


def f64(x):
    return np.asarray(x).astype(np.float64)


def striped(idx):
    return np.tile(idx.reshape(-1, 16).T, (8, 1)).astype(np.uint16)


def unstriped(offs):
    return offs[:16].T.reshape(-1).astype(np.int64)


def striped8(idx):
    return np.concatenate([x.reshape(-1, 16).T for x in idx]).astype(np.uint16)


def runs(offs, k):
    lists = np.stack([offs[16 * r : 16 * r + 16].T.reshape(-1) for r in range(8)]).astype(np.int64)
    return lists[np.arange(k) % 512 // 64]


def pack_weight(w):
    k, n = w.shape
    w = f64(np.asarray(w, np.float32).astype(ml_dtypes.bfloat16)).reshape(k // 32, 32, n)
    amax = np.abs(w).max(1)
    byte = np.clip(np.where(amax > 0, np.frexp(amax)[1] - 1 + 127 - 7, 1), 1, 254)
    scaled = (w * np.exp2(127.0 - byte)[:, None, :]).reshape(k, n).astype(np.float32)
    words = np.ascontiguousarray(scaled.reshape(k // 512, 128, 4, n).transpose(0, 1, 3, 2)).astype(ml_dtypes.float8_e4m3fn).view(np.uint8)
    return words, np.ascontiguousarray(byte.astype(np.uint8).reshape(k // 512, 16, n))


def unpack_weight(words, scales):
    g, p, n, _ = words.shape
    vals = np.ascontiguousarray(words).view(ml_dtypes.float8_e4m3fn).astype(np.float64) * np.repeat(np.exp2(scales.astype(np.float64) - 127.0), 8, axis=1)[..., None]
    return vals.transpose(0, 1, 3, 2).reshape(g * 512, n)


def relu(v):
    return np.maximum(v, 0.0)

def planes(y):
    n, m = y.shape
    v = y.astype(np.float32).astype(ml_dtypes.bfloat16).astype(np.float64).reshape(n // 32, 32, m)
    top = np.abs(v).max(1)
    byte = np.clip(np.where(top > 0, np.frexp(top)[1] - 1 + 127 - 7, 1), 1, 254)
    codes = (v * np.exp2(127.0 - byte)[:, None, :]).reshape(n, m).astype(np.float32).astype(ml_dtypes.float8_e4m3fn).view(np.uint8)
    words = codes.reshape(n // 512, 128, 4, m).transpose(0, 1, 3, 2)
    return np.ascontiguousarray(words), np.ascontiguousarray(byte.astype(np.uint8).reshape(n // 512, 16, m))


K, T, S, V, N, H = 512, 2048, 512, 256, 512, 512


def setup_inputs():
    n = np.random.standard_normal
    s = mx_kscale(K)[:, None]
    u = mx_kscale(H)
    packed_xT = pack_weight(n((K, T)) * s)
    packed_w3 = pack_weight(n((H, N)) / np.sqrt(2 * H) / u[:, None])
    packed_w4 = pack_weight(n((H, N)) / np.sqrt(2 * H) / u[:, None])
    return {
        "x_words": packed_xT[0],
        "x_scales": packed_xT[1],
        "w1": (n((K, H)) / np.sqrt(K) / s * u).astype(np.float32),
        "wt": np.repeat(np.random.uniform(0.3, 1.2, (8, V)), 64, axis=0).astype(np.float32),
        "w2": (n((K, H)) / np.sqrt(K) / s * u).astype(np.float32),
        "w3_words": packed_w3[0],
        "w3_scales": packed_w3[1],
        "w4_words": packed_w4[0],
        "w4_scales": packed_w4[1],
        "offs": striped(np.random.permutation(T)[:S]),
        "take": striped8(np.stack([np.random.permutation(S)[:V] for _ in range(8)])),
    }


def reference(x_words, x_scales, w1, wt, w2, w3_words, w3_scales, w4_words, w4_scales, offs, take):
    xq = unpack_weight(x_words, x_scales)[:, unstriped(offs)]
    y = mxq(f64(w1), 0, "e4m3").T @ xq
    e = (relu(y[np.arange(H)[:, None], runs(take, H)])) * f64(wt)
    z = np.zeros((H, S))
    z[np.arange(H)[:, None], runs(take, H)] = e
    z2 = relu(mxq(f64(w2), 0, "e4m3").T @ xq)
    out_0 = unpack_weight(w3_words, w3_scales).T @ mxq(z, 0, "e4m3") + unpack_weight(w4_words, w4_scales).T @ mxq(z2, 0, "e4m3")
    return (out_0,) + planes(out_0)

@@ -1,0 +1,237 @@
+from contextlib import ExitStack
+
+import concourse.mybir as mybir
+
+FLOPS = 4 * 2 * 512 * 512 * 512
+
+F32 = mybir.dt.float32
+BF16 = mybir.dt.bfloat16
+I32 = mybir.dt.int32
+U32 = mybir.dt.uint32
+U16 = mybir.dt.uint16
+U8 = mybir.dt.uint8
+FP8X4 = mybir.dt.float8_e4m3fn_x4
+RELU = mybir.ActivationFunctionType.Relu
+MULT = mybir.AluOpType.mult
+
+P = 128
+PACK = 4
+T = 2048
+S = 512
+V = 256
+H = 512
+HALF = 256
+CHUNK = 128
+W1_VECTOR_M = 88
+
+
+def as_words(packed):
+    return packed[0].rearrange("p n r -> p (n r)").bitcast(I32)
+
+
+def tile_picked_sharedexp_relu_po_kernel(
+    tc, x_words, x_scales, w1, wt, w2, w3_words, w3_scales, w4_words, w4_scales, offs, take, out_0, out_1, out_2
+):
+    nc = tc.nc
+    with ExitStack() as ctx:
+        sb = ctx.enter_context(tc.tile_pool(name="sb", bufs=1))
+        psum = ctx.enter_context(tc.psum_pool(name="psum", bufs=1))
+
+        def tile(name, shape, dtype, after=None):
+            return sb.tile(shape, dtype, name=name, tag=after or name, align_bytes=64)
+
+        def bank(b, shape):
+            return psum.tile(shape, F32, name="bank%d" % b, tag="bank%d" % b)
+
+        offs_sb = tile("offs_sb", [P, S // 16], U16)
+        take_sb = tile("take_sb", [P, V // 16], U16)
+        x_table = tile("x_table", [P, T], U32)
+        x_table_scales = tile("x_table_scales", [P, T], U8)
+        w1_raw = tile("w1_raw", [P, PACK, H], F32)
+        w2_raw = tile("w2_raw", [P, PACK, H], F32)
+        wt_sb = tile("wt_sb", [P, V], F32)
+        w3_raw = tile("w3_raw", [P, H], I32)
+        w4_raw = tile("w4_raw", [P, H], I32)
+        w34_raw_scales = tile("w34_raw_scales", [P, H], U8)
+        z_rows = [tile("z_rows%d" % t, [P, S], F32) for t in range(PACK)]
+
+        nc.vector.memset(x_table_scales[:].bitcast(I32), 0)
+        nc.vector.memset(w34_raw_scales[:].bitcast(I32), 0)
+        for t in range(PACK):
+            nc.vector.memset(z_rows[t][:], 0.0)
+
+        nc.sync.dma_start(w1_raw[:], w1.rearrange("(p j) c -> p j c", j=PACK))
+        nc.sync.dma_start(offs_sb[:], offs)
+        for q in range(4):
+            nc.scalar.dma_start(x_table_scales[32 * q : 32 * q + 4, :].bitcast(I32), x_scales[0, 4 * q : 4 * q + 4, :].bitcast(I32))
+        nc.sync.dma_start(x_table[:].bitcast(I32), as_words(x_words))
+        nc.sync.dma_start(take_sb[:], take)
+        nc.sync.dma_start(wt_sb[:], wt.rearrange("(p j) v -> p j v", j=PACK)[:, 0, :])
+        nc.sync.dma_start(w4_raw[:], as_words(w4_words))
+        nc.sync.dma_start(w2_raw[:], w2.rearrange("(p j) c -> p j c", j=PACK))
+        nc.sync.dma_start(w3_raw[:], as_words(w3_words))
+        for first, scales in ((0, w3_scales), (4, w4_scales)):
+            for q in range(4):
+                nc.sync.dma_start(
+                    w34_raw_scales[32 * q + first : 32 * q + first + 4, :].bitcast(I32), scales[0, 4 * q : 4 * q + 4, :].bitcast(I32)
+                )
+
+        def deal_view(dealt, raw, ms):
+            return (
+                dealt[:].rearrange("p t m j -> p m j t")[:, ms],
+                raw[:].rearrange("p j (m t) -> p m j t", t=PACK)[:, ms],
+            )
+
+        def quantize(name, grouped, cols):
+            codes = tile(name + "_codes", [P, cols], U32)
+            scales = tile(name + "_scales", [P, cols], U8)
+            nc.vector.quantize_mx(out=codes[:].bitcast(FP8X4), scales=scales[:], in_=grouped)
+            return codes, scales
+
+        xg_scales = tile("xg_scales", [P, S], U8)
+        nc.vector.tensor_copy(xg_scales[:], x_table_scales[:].indirect(offs_sb[:]))
+
+        w1_bf = tile("w1_bf", [P, PACK, P, PACK], BF16)
+        nc.vector.tensor_copy(*deal_view(w1_bf, w1_raw, slice(0, W1_VECTOR_M)))
+        nc.scalar.copy(*deal_view(w1_bf, w1_raw, slice(W1_VECTOR_M, P)))
+        w1_codes, w1_scales = quantize("w1", w1_bf[:].rearrange("p t m j -> p (t m j)"), H)
+
+        xg = [tile("xg%d" % h, [P, HALF], U32) for h in range(2)]
+        for h in range(2):
+            nc.vector.tensor_copy(xg[h][:], x_table[:].indirect(offs_sb[:, h * 16 : (h + 1) * 16]))
+
+        y_rows = [tile("y_rows%d" % t, [P, S], F32) for t in range(PACK)]
+        for t in range(PACK):
+            for h in range(2):
+                acc = bank(2 * t + h, [P, HALF])
+                nc.tensor.matmul_mx(
+                    acc[:],
+                    lhsT=w1_codes[:, t * P : (t + 1) * P].bitcast(FP8X4),
+                    lhsT_scale=w1_scales[:, t * P : (t + 1) * P],
+                    rhs=xg[h][:].bitcast(FP8X4),
+                    rhs_scale=xg_scales[:, h * HALF : (h + 1) * HALF],
+                    start=True,
+                    stop=True,
+                )
+                nc.scalar.activation(y_rows[t][:, h * HALF : (h + 1) * HALF], acc[:], RELU)
+
+        def deal_words(dealt, raw, ms):
+            nc.vector.tensor_copy(dealt[:].rearrange("p t m -> p m t")[:, ms], raw[:].rearrange("p (m t) -> p m t", t=PACK)[:, ms])
+
+        w4_codes = tile("w4_codes", [P, PACK, P], I32)
+        deal_words(w4_codes, w4_raw, slice(0, P))
+
+        def gather(t, after=None):
+            picked = tile("picked%d" % t, [P, V], F32, after)
+            nc.vector.tensor_copy(picked[:], y_rows[t][:].indirect(take_sb[:]))
+            return picked
+
+        def scatter(t, picked):
+            nc.vector.tensor_tensor(z_rows[t][:].indirect(take_sb[:]), picked[:], wt_sb[:], MULT)
+
+        def interleave(engine_copy, grouped, planes):
+            engine_copy(grouped[:].rearrange("p (c i) t -> p c t i", i=4), planes[:].rearrange("p t (c i) -> p c t i", i=4))
+
+        picked0 = gather(0)
+        picked1 = gather(1)
+        scatter(0, picked0)
+        scatter(1, picked1)
+
+        w2_bf = [tile("w2_bf%d" % u, [P, 2, P, PACK], BF16) for u in range(2)]
+        w2_codes = tile("w2_codes", [P, H], U32)
+        w2_scales = tile("w2_scales", [P, H], U8)
+        for u in range(2):
+            nc.scalar.copy(
+                w2_bf[u][:].rearrange("p t m j -> p m j t"), w2_raw[:].rearrange("p j (m t) -> p m j t", t=PACK)[:, :, :, 2 * u : 2 * u + 2]
+            )
+        for u in range(2):
+            nc.vector.quantize_mx(
+                out=w2_codes[:, u * HALF : (u + 1) * HALF].bitcast(FP8X4),
+                scales=w2_scales[:, u * HALF : (u + 1) * HALF],
+                in_=w2_bf[u][:].rearrange("p t m j -> p (t m j)"),
+            )
+        w34_scales = tile("w34_scales", [P, PACK, P], U8, "w2_bf0")
+        nc.vector.tensor_copy(w34_scales[:], w34_raw_scales[:].rearrange("p (m t) -> p t m", t=PACK))
+
+        z2_bf = [tile("z2_bf%d" % h, [P, HALF, PACK], BF16) for h in range(2)]
+        for c in range(S // CHUNK):
+            acc = bank(c, [P, PACK, CHUNK])
+            h, c0 = divmod(c * CHUNK, HALF)
+            for t in range(PACK):
+                nc.tensor.matmul_mx(
+                    acc[:, t, :],
+                    lhsT=w2_codes[:, t * P : (t + 1) * P].bitcast(FP8X4),
+                    lhsT_scale=w2_scales[:, t * P : (t + 1) * P],
+                    rhs=xg[h][:, c0 : c0 + CHUNK].bitcast(FP8X4),
+                    rhs_scale=xg_scales[:, c * CHUNK : (c + 1) * CHUNK],
+                    start=True,
+                    stop=True,
+                )
+            nc.scalar.activation(z2_bf[h][:, c0 : c0 + CHUNK, :], acc[:].rearrange("p t n -> p n t"), RELU)
+
+        picked2 = gather(2, "w2_bf1")
+        scatter(2, picked2)
+
+        out_acc = [[bank(PACK * (1 - h) + t, [P, HALF]) for t in range(PACK)] for h in range(2)]
+
+        def shared_expert_passes(h):
+            z2_codes, z2_scales = quantize("z2_%d" % h, z2_bf[h][:].rearrange("p n t -> p (n t)"), HALF)
+            for t in range(PACK):
+                nc.tensor.matmul_mx(
+                    out_acc[h][t][:],
+                    lhsT=w4_codes[:, t, :].bitcast(FP8X4),
+                    lhsT_scale=w34_scales[4:P, t, :],
+                    rhs=z2_codes[:].bitcast(FP8X4),
+                    rhs_scale=z2_scales[:],
+                    start=True,
+                    stop=False,
+                )
+
+        shared_expert_passes(0)
+        picked3 = gather(3, "z2_bf0")
+        w3_codes = tile("w3_codes", [P, PACK, P], I32, "y_rows3")
+        deal_words(w3_codes, w3_raw, slice(0, P))
+        scatter(3, picked3)
+        shared_expert_passes(1)
+
+        z_planes = [tile("z_planes%d" % h, [P, PACK, HALF], BF16, ("w2_codes", "w2_scales")[h]) for h in range(2)]
+        for t in range(PACK):
+            for h in range(2):
+                copy = nc.vector.tensor_copy if (t, h) == (PACK - 1, 0) else nc.scalar.copy
+                copy(z_planes[h][:, t, :], z_rows[t][:, h * HALF : (h + 1) * HALF])
+
+        out_rows = out_0.rearrange("(p t) n -> p t n", t=PACK)
+        out_words = as_words(out_1)
+        out_scales = tile("out_scales", [P, S], U8)
+        out_f32 = [tile("out_f32_%d" % h, [P, PACK, HALF], F32) for h in range(2)]
+        z_bf = [tile("z_bf%d" % h, [P, HALF, PACK], BF16) for h in range(2)]
+        interleave(nc.vector.tensor_copy, z_bf[0], z_planes[0])
+        interleave(nc.scalar.copy, z_bf[1], z_planes[1])
+        for h in range(2):
+            z_codes, z_scales = quantize("z%d" % h, z_bf[h][:].rearrange("p n t -> p (n t)"), HALF)
+            for t in range(PACK):
+                nc.tensor.matmul_mx(
+                    out_acc[h][t][:],
+                    lhsT=w3_codes[:, t, :].bitcast(FP8X4),
+                    lhsT_scale=w34_scales[:, t, :],
+                    rhs=z_codes[:].bitcast(FP8X4),
+                    rhs_scale=z_scales[:],
+                    start=False,
+                    stop=True,
+                )
+        for h in range(2):
+            cols = slice(h * HALF, (h + 1) * HALF)
+            for t in range(PACK):
+                if h == 0 and t % 2 == 1:
+                    nc.vector.tensor_copy(out_f32[h][:, t, :], out_acc[h][t][:])
+                else:
+                    nc.scalar.copy(out_f32[h][:, t, :], out_acc[h][t][:])
+            nc.sync.dma_start(out_rows[:, :, cols], out_f32[h][:])
+            out_bf = tile("out_bf%d" % h, [P, HALF, PACK], BF16)
+            interleave(nc.vector.tensor_copy, out_bf, out_f32[h])
+            out_codes = tile("out_codes%d" % h, [P, HALF], U32)
+            nc.vector.quantize_mx(out=out_codes[:].bitcast(FP8X4), scales=out_scales[:, cols], in_=out_bf[:].rearrange("p n t -> p (n t)"))
+            nc.sync.dma_start(out_words[:, cols], out_codes[:].bitcast(I32))
+        for q in range(4):
+            queue = nc.sync if q < 2 else nc.scalar
+            queue.dma_start(out_2[0, 4 * q : 4 * q + 4, :].bitcast(I32), out_scales[32 * q : 32 * q + 4, :].bitcast(I32))

@@ -22,7 +22,7 @@ V = 256
 H = 512
 HALF = 256
 CHUNK = 128
-W1_VECTOR_M = 88
+W1_VECTOR_M = 32
 
 
 def as_words(packed):
@@ -35,10 +35,14 @@ def tile_picked_sharedexp_relu_po_kernel(
     nc = tc.nc
     with ExitStack() as ctx:
         sb = ctx.enter_context(tc.tile_pool(name="sb", bufs=1))
+        placed = ctx.enter_context(tc.tile_pool(name="placed", bufs=1))
         psum = ctx.enter_context(tc.psum_pool(name="psum", bufs=1))
 
         def tile(name, shape, dtype, after=None):
             return sb.tile(shape, dtype, name=name, tag=after or name, align_bytes=64)
+
+        def placed_tile(name, shape, dtype, offset):
+            return placed.tile(shape, dtype, name=name, align_bytes=64, offset=offset)
 
         def bank(b, shape):
             return psum.tile(shape, F32, name="bank%d" % b, tag="bank%d" % b)
@@ -48,7 +52,7 @@ def tile_picked_sharedexp_relu_po_kernel(
         x_table = tile("x_table", [P, T], U32)
         x_table_scales = tile("x_table_scales", [P, T], U8)
         w1_raw = tile("w1_raw", [P, PACK, H], F32)
-        w2_raw = tile("w2_raw", [P, PACK, H], F32)
+        w2_raw = [tile("w2_raw0", [P, PACK, HALF], F32), placed_tile("w2_raw1", [P, PACK, HALF], F32, 1024)]
         wt_sb = tile("wt_sb", [P, V], F32)
         w3_raw = tile("w3_raw", [P, H], I32)
         w4_raw = tile("w4_raw", [P, H], I32)
@@ -60,21 +64,25 @@ def tile_picked_sharedexp_relu_po_kernel(
         for t in range(PACK):
             nc.vector.memset(z_rows[t][:], 0.0)
 
-        nc.sync.dma_start(w1_raw[:], w1.rearrange("(p j) c -> p j c", j=PACK))
+        def load_scales(plane, first, scales):
+            for r in range(4):
+                nc.sync.dma_start(plane[first + r : P : 32, :].bitcast(I32), scales[0, r:16:4, :].bitcast(I32))
+
+        def load_w2(u):
+            nc.sync.dma_start(w2_raw[u][:], w2.rearrange("(p j) c -> p j c", j=PACK)[:, :, u * HALF : (u + 1) * HALF])
+
         nc.sync.dma_start(offs_sb[:], offs)
-        for q in range(4):
-            nc.scalar.dma_start(x_table_scales[32 * q : 32 * q + 4, :].bitcast(I32), x_scales[0, 4 * q : 4 * q + 4, :].bitcast(I32))
-        nc.sync.dma_start(x_table[:].bitcast(I32), as_words(x_words))
         nc.sync.dma_start(take_sb[:], take)
+        nc.sync.dma_start(w1_raw[:], w1.rearrange("(p j) c -> p j c", j=PACK))
+        load_scales(x_table_scales, 0, x_scales)
+        nc.sync.dma_start(x_table[:].bitcast(I32), as_words(x_words))
         nc.sync.dma_start(wt_sb[:], wt.rearrange("(p j) v -> p j v", j=PACK)[:, 0, :])
         nc.sync.dma_start(w4_raw[:], as_words(w4_words))
-        nc.sync.dma_start(w2_raw[:], w2.rearrange("(p j) c -> p j c", j=PACK))
+        load_w2(0)
+        load_scales(w34_raw_scales, 4, w4_scales)
+        load_w2(1)
+        load_scales(w34_raw_scales, 0, w3_scales)
         nc.sync.dma_start(w3_raw[:], as_words(w3_words))
-        for first, scales in ((0, w3_scales), (4, w4_scales)):
-            for q in range(4):
-                nc.sync.dma_start(
-                    w34_raw_scales[32 * q + first : 32 * q + first + 4, :].bitcast(I32), scales[0, 4 * q : 4 * q + 4, :].bitcast(I32)
-                )
 
         def deal_view(dealt, raw, ms):
             return (
@@ -100,12 +108,12 @@ def tile_picked_sharedexp_relu_po_kernel(
         for h in range(2):
             nc.vector.tensor_copy(xg[h][:], x_table[:].indirect(offs_sb[:, h * 16 : (h + 1) * 16]))
 
-        y_rows = [tile("y_rows%d" % t, [P, S], F32) for t in range(PACK)]
+        y_rows = [tile("y_rows0", [P, S], F32)] + [placed_tile("y_rows%d" % t, [P, S], F32, 2048 * (t - 1)) for t in range(1, PACK)]
+        y_acc = [[bank(2 * t + h, [P, HALF]) for h in range(2)] for t in range(PACK)]
         for t in range(PACK):
             for h in range(2):
-                acc = bank(2 * t + h, [P, HALF])
                 nc.tensor.matmul_mx(
-                    acc[:],
+                    y_acc[t][h][:],
                     lhsT=w1_codes[:, t * P : (t + 1) * P].bitcast(FP8X4),
                     lhsT_scale=w1_scales[:, t * P : (t + 1) * P],
                     rhs=xg[h][:].bitcast(FP8X4),
@@ -113,47 +121,53 @@ def tile_picked_sharedexp_relu_po_kernel(
                     start=True,
                     stop=True,
                 )
-                nc.scalar.activation(y_rows[t][:, h * HALF : (h + 1) * HALF], acc[:], RELU)
 
-        def deal_words(dealt, raw, ms):
-            nc.vector.tensor_copy(dealt[:].rearrange("p t m -> p m t")[:, ms], raw[:].rearrange("p (m t) -> p m t", t=PACK)[:, ms])
+        def relu_y(t):
+            for h in range(2):
+                rows = y_rows[t][:, h * HALF : (h + 1) * HALF]
+                if t == 0:
+                    nc.vector.tensor_scalar_max(rows, y_acc[t][h][:], 0.0)
+                else:
+                    nc.scalar.activation(rows, y_acc[t][h][:], RELU)
 
-        w4_codes = tile("w4_codes", [P, PACK, P], I32)
-        deal_words(w4_codes, w4_raw, slice(0, P))
+        def deal_words(dealt, raw):
+            nc.vector.tensor_copy(dealt[:].rearrange("p t m -> p m t"), raw[:].rearrange("p (m t) -> p m t", t=PACK))
 
-        def gather(t, after=None):
-            picked = tile("picked%d" % t, [P, V], F32, after)
+        def gather(t, picked):
             nc.vector.tensor_copy(picked[:], y_rows[t][:].indirect(take_sb[:]))
-            return picked
 
         def scatter(t, picked):
             nc.vector.tensor_tensor(z_rows[t][:].indirect(take_sb[:]), picked[:], wt_sb[:], MULT)
 
-        def interleave(engine_copy, grouped, planes):
-            engine_copy(grouped[:].rearrange("p (c i) t -> p c t i", i=4), planes[:].rearrange("p t (c i) -> p c t i", i=4))
-
-        picked0 = gather(0)
-        picked1 = gather(1)
+        relu_y(0)
+        w4_codes = tile("w4_codes", [P, PACK, P], I32)
+        deal_words(w4_codes, w4_raw)
+        picked0 = tile("picked0", [P, V], F32)
+        gather(0, picked0)
+        w34_scales = tile("w34_scales", [P, PACK, P], U8, "y_rows0")
+        nc.vector.tensor_copy(w34_scales[:], w34_raw_scales[:].rearrange("p (m t) -> p t m", t=PACK))
         scatter(0, picked0)
-        scatter(1, picked1)
 
-        w2_bf = [tile("w2_bf%d" % u, [P, 2, P, PACK], BF16) for u in range(2)]
-        w2_codes = tile("w2_codes", [P, H], U32)
-        w2_scales = tile("w2_scales", [P, H], U8)
+        w2_bf = tile("w2_bf", [P, PACK, P, PACK], BF16)
         for u in range(2):
             nc.scalar.copy(
-                w2_bf[u][:].rearrange("p t m j -> p m j t"), w2_raw[:].rearrange("p j (m t) -> p m j t", t=PACK)[:, :, :, 2 * u : 2 * u + 2]
+                w2_bf[:].rearrange("p t m j -> p m j t")[:, u * 64 : (u + 1) * 64], w2_raw[u][:].rearrange("p j (m t) -> p m j t", t=PACK)
             )
-        for u in range(2):
-            nc.vector.quantize_mx(
-                out=w2_codes[:, u * HALF : (u + 1) * HALF].bitcast(FP8X4),
-                scales=w2_scales[:, u * HALF : (u + 1) * HALF],
-                in_=w2_bf[u][:].rearrange("p t m j -> p (t m j)"),
-            )
-        w34_scales = tile("w34_scales", [P, PACK, P], U8, "w2_bf0")
-        nc.vector.tensor_copy(w34_scales[:], w34_raw_scales[:].rearrange("p (m t) -> p t m", t=PACK))
+        for t in range(1, PACK):
+            relu_y(t)
+        w2_codes, w2_scales = quantize("w2", w2_bf[:].rearrange("p t m j -> p (t m j)"), H)
+        picked1 = tile("picked1", [P, V], F32)
+        picked2 = tile("picked2", [P, V], F32)
+        gather(1, picked1)
+        gather(2, picked2)
+        scatter(1, picked1)
+        scatter(2, picked2)
+        w3_codes = tile("w3_codes", [P, PACK, P], I32, "picked2")
+        deal_words(w3_codes, w3_raw)
 
-        z2_bf = [tile("z2_bf%d" % h, [P, HALF, PACK], BF16) for h in range(2)]
+        z2_bf = tile("z2_bf", [P, S, PACK], BF16)
+        zero_bias = tile("zero_bias", [P, 1], F32)
+        nc.vector.memset(zero_bias[:], 0.0)
         for c in range(S // CHUNK):
             acc = bank(c, [P, PACK, CHUNK])
             h, c0 = divmod(c * CHUNK, HALF)
@@ -167,46 +181,36 @@ def tile_picked_sharedexp_relu_po_kernel(
                     start=True,
                     stop=True,
                 )
-            nc.scalar.activation(z2_bf[h][:, c0 : c0 + CHUNK, :], acc[:].rearrange("p t n -> p n t"), RELU)
+            nc.scalar.activation(z2_bf[:, c * CHUNK : (c + 1) * CHUNK, :], acc[:].rearrange("p t n -> p n t"), RELU, bias=zero_bias[:])
 
-        picked2 = gather(2, "w2_bf1")
-        scatter(2, picked2)
+        z_bf = [tile("z_bf%d" % h, [P, HALF, PACK], BF16, ("w2_codes", "w2_scales")[h]) for h in range(2)]
 
+        def round_z(t, h):
+            copy = nc.vector.tensor_copy if t >= 2 and h == 0 else nc.scalar.copy
+            copy(z_bf[h][:, :, t], z_rows[t][:, h * HALF : (h + 1) * HALF])
+
+        for h in range(2):
+            for t in range(3):
+                round_z(t, h)
+
+        picked3 = tile("picked3", [P, V], F32, "zero_bias")
+        gather(3, picked3)
+        z2_codes, z2_scales = quantize("z2", z2_bf[:].rearrange("p n t -> p (n t)"), S)
         out_acc = [[bank(PACK * (1 - h) + t, [P, HALF]) for t in range(PACK)] for h in range(2)]
-
-        def shared_expert_passes(h):
-            z2_codes, z2_scales = quantize("z2_%d" % h, z2_bf[h][:].rearrange("p n t -> p (n t)"), HALF)
+        for h in range(2):
             for t in range(PACK):
                 nc.tensor.matmul_mx(
                     out_acc[h][t][:],
                     lhsT=w4_codes[:, t, :].bitcast(FP8X4),
                     lhsT_scale=w34_scales[4:P, t, :],
-                    rhs=z2_codes[:].bitcast(FP8X4),
-                    rhs_scale=z2_scales[:],
+                    rhs=z2_codes[:, h * HALF : (h + 1) * HALF].bitcast(FP8X4),
+                    rhs_scale=z2_scales[:, h * HALF : (h + 1) * HALF],
                     start=True,
                     stop=False,
                 )
-
-        shared_expert_passes(0)
-        picked3 = gather(3, "z2_bf0")
-        w3_codes = tile("w3_codes", [P, PACK, P], I32, "y_rows3")
-        deal_words(w3_codes, w3_raw, slice(0, P))
         scatter(3, picked3)
-        shared_expert_passes(1)
-
-        z_planes = [tile("z_planes%d" % h, [P, PACK, HALF], BF16, ("w2_codes", "w2_scales")[h]) for h in range(2)]
-        for t in range(PACK):
-            for h in range(2):
-                copy = nc.vector.tensor_copy if (t, h) == (PACK - 1, 0) else nc.scalar.copy
-                copy(z_planes[h][:, t, :], z_rows[t][:, h * HALF : (h + 1) * HALF])
-
-        out_rows = out_0.rearrange("(p t) n -> p t n", t=PACK)
-        out_words = as_words(out_1)
-        out_scales = tile("out_scales", [P, S], U8)
-        out_f32 = [tile("out_f32_%d" % h, [P, PACK, HALF], F32) for h in range(2)]
-        z_bf = [tile("z_bf%d" % h, [P, HALF, PACK], BF16) for h in range(2)]
-        interleave(nc.vector.tensor_copy, z_bf[0], z_planes[0])
-        interleave(nc.scalar.copy, z_bf[1], z_planes[1])
+        for h in range(2):
+            round_z(3, h)
         for h in range(2):
             z_codes, z_scales = quantize("z%d" % h, z_bf[h][:].rearrange("p n t -> p (n t)"), HALF)
             for t in range(PACK):
@@ -219,19 +223,42 @@ def tile_picked_sharedexp_relu_po_kernel(
                     start=False,
                     stop=True,
                 )
+
+        out_rows = out_0.rearrange("(p t) n -> p t n", t=PACK)
+        out_words = as_words(out_1)
+        out_scales = tile("out_scales", [P, S], U8)
+        out_f32 = [tile("out_f32_%d" % h, [P, PACK, HALF], F32) for h in range(2)]
+        out_codes = [tile("out_codes%d" % h, [P, HALF], U32) for h in range(2)]
+
+        def round_out(copy, h, first, count):
+            rounded = tile("out_bf%d_%d" % (h, first), [P, count, PACK], BF16)
+            copy(
+                rounded[:].rearrange("p (c i) t -> p c t i", i=4),
+                out_f32[h][:, :, first : first + count].rearrange("p t (c i) -> p c t i", i=4),
+            )
+            return rounded
+
+        def quantize_out(rounded, h, first, count):
+            nc.vector.quantize_mx(
+                out=out_codes[h][:, first : first + count].bitcast(FP8X4),
+                scales=out_scales[:, h * HALF + first : h * HALF + first + count],
+                in_=rounded[:].rearrange("p n t -> p (n t)"),
+            )
+
         for h in range(2):
             cols = slice(h * HALF, (h + 1) * HALF)
             for t in range(PACK):
-                if h == 0 and t % 2 == 1:
-                    nc.vector.tensor_copy(out_f32[h][:, t, :], out_acc[h][t][:])
-                else:
-                    nc.scalar.copy(out_f32[h][:, t, :], out_acc[h][t][:])
-            nc.sync.dma_start(out_rows[:, :, cols], out_f32[h][:])
-            out_bf = tile("out_bf%d" % h, [P, HALF, PACK], BF16)
-            interleave(nc.vector.tensor_copy, out_bf, out_f32[h])
-            out_codes = tile("out_codes%d" % h, [P, HALF], U32)
-            nc.vector.quantize_mx(out=out_codes[:].bitcast(FP8X4), scales=out_scales[:, cols], in_=out_bf[:].rearrange("p n t -> p (n t)"))
-            nc.sync.dma_start(out_words[:, cols], out_codes[:].bitcast(I32))
-        for q in range(4):
-            queue = nc.sync if q < 2 else nc.scalar
-            queue.dma_start(out_2[0, 4 * q : 4 * q + 4, :].bitcast(I32), out_scales[32 * q : 32 * q + 4, :].bitcast(I32))
+                copy = nc.vector.tensor_copy if h == 0 and t % 2 == 1 else nc.scalar.copy
+                copy(out_f32[h][:, t, :], out_acc[h][t][:])
+                if t % 2 == 1:
+                    nc.sync.dma_start(out_rows[:, t - 1 : t + 1, cols], out_f32[h][:, t - 1 : t + 1, :])
+        quantize_out(round_out(nc.vector.tensor_copy, 0, 0, HALF), 0, 0, HALF)
+        nc.sync.dma_start(out_words[:, :HALF], out_codes[0][:].bitcast(I32))
+        by_vector = round_out(nc.vector.tensor_copy, 1, 0, CHUNK)
+        by_scalar = round_out(nc.scalar.copy, 1, CHUNK, CHUNK)
+        quantize_out(by_scalar, 1, CHUNK, CHUNK)
+        quantize_out(by_vector, 1, 0, CHUNK)
+        nc.sync.dma_start(out_words[:, HALF:], out_codes[1][:].bitcast(I32))
+        for r in range(4):
+            queue = nc.sync if r < 2 else nc.scalar
+            queue.dma_start(out_2[0, r:16:4, :].bitcast(I32), out_scales[r:P:32, :].bitcast(I32))

@@ -23,6 +23,7 @@ H = 512
 HALF = 256
 CHUNK = 128
 W1_VECTOR_M = 32
+ORDER = (2, 0, 1, 3)
 
 
 def as_words(packed):
@@ -57,7 +58,7 @@ def tile_picked_sharedexp_relu_po_kernel(
         w3_raw = tile("w3_raw", [P, H], I32)
         w4_raw = tile("w4_raw", [P, H], I32)
         w34_raw_scales = tile("w34_raw_scales", [P, H], U8)
-        z_rows = [tile("z_rows%d" % t, [P, S], F32) for t in range(PACK)]
+        z_rows = [placed_tile("z_rows2", [P, S], F32, 10240) if t == 2 else tile("z_rows%d" % t, [P, S], F32) for t in range(PACK)]
 
         nc.vector.memset(x_table_scales[:].bitcast(I32), 0)
         nc.vector.memset(w34_raw_scales[:].bitcast(I32), 0)
@@ -76,13 +77,13 @@ def tile_picked_sharedexp_relu_po_kernel(
         nc.sync.dma_start(w1_raw[:], w1.rearrange("(p j) c -> p j c", j=PACK))
         load_scales(x_table_scales, 0, x_scales)
         nc.sync.dma_start(x_table[:].bitcast(I32), as_words(x_words))
-        nc.sync.dma_start(wt_sb[:], wt.rearrange("(p j) v -> p j v", j=PACK)[:, 0, :])
-        nc.sync.dma_start(w4_raw[:], as_words(w4_words))
         load_w2(0)
-        load_scales(w34_raw_scales, 4, w4_scales)
+        nc.sync.dma_start(wt_sb[:], wt.rearrange("(p j) v -> p j v", j=PACK)[:, 0, :])
         load_w2(1)
-        load_scales(w34_raw_scales, 0, w3_scales)
+        nc.sync.dma_start(w4_raw[:], as_words(w4_words))
         nc.sync.dma_start(w3_raw[:], as_words(w3_words))
+        load_scales(w34_raw_scales, 4, w4_scales)
+        load_scales(w34_raw_scales, 0, w3_scales)
 
         def deal_view(dealt, raw, ms):
             return (
@@ -102,15 +103,30 @@ def tile_picked_sharedexp_relu_po_kernel(
         w1_bf = tile("w1_bf", [P, PACK, P, PACK], BF16)
         nc.vector.tensor_copy(*deal_view(w1_bf, w1_raw, slice(0, W1_VECTOR_M)))
         nc.scalar.copy(*deal_view(w1_bf, w1_raw, slice(W1_VECTOR_M, P)))
-        w1_codes, w1_scales = quantize("w1", w1_bf[:].rearrange("p t m j -> p (t m j)"), H)
+        w1_codes = tile("w1_codes", [P, H], U32)
+        w1_scales = tile("w1_scales", [P, H], U8)
+
+        def quantize_w1(t0, t1):
+            nc.vector.quantize_mx(
+                out=w1_codes[:, t0 * P : t1 * P].bitcast(FP8X4),
+                scales=w1_scales[:, t0 * P : t1 * P],
+                in_=w1_bf[:, t0:t1].rearrange("p t m j -> p (t m j)"),
+            )
+
+        quantize_w1(2, 3)
 
         xg = [tile("xg%d" % h, [P, HALF], U32) for h in range(2)]
         for h in range(2):
             nc.vector.tensor_copy(xg[h][:], x_table[:].indirect(offs_sb[:, h * 16 : (h + 1) * 16]))
+        quantize_w1(0, 2)
+        quantize_w1(3, 4)
 
-        y_rows = [tile("y_rows0", [P, S], F32)] + [placed_tile("y_rows%d" % t, [P, S], F32, 2048 * (t - 1)) for t in range(1, PACK)]
-        y_acc = [[bank(2 * t + h, [P, HALF]) for h in range(2)] for t in range(PACK)]
-        for t in range(PACK):
+        first, second, third, last = ORDER
+        y_rows = {first: tile("y_rows_first", [P, S], F32)}
+        for i, t in enumerate(ORDER[1:]):
+            y_rows[t] = placed_tile("y_rows%d" % t, [P, S], F32, 2048 * i)
+        y_acc = {t: [bank(2 * i + h, [P, HALF]) for h in range(2)] for i, t in enumerate(ORDER)}
+        for t in ORDER:
             for h in range(2):
                 nc.tensor.matmul_mx(
                     y_acc[t][h][:],
@@ -125,13 +141,13 @@ def tile_picked_sharedexp_relu_po_kernel(
         def relu_y(t):
             for h in range(2):
                 rows = y_rows[t][:, h * HALF : (h + 1) * HALF]
-                if t == 0:
+                if t == first:
                     nc.vector.tensor_scalar_max(rows, y_acc[t][h][:], 0.0)
                 else:
                     nc.scalar.activation(rows, y_acc[t][h][:], RELU)
 
         def deal_words(dealt, raw):
-            nc.vector.tensor_copy(dealt[:].rearrange("p t m -> p m t"), raw[:].rearrange("p (m t) -> p m t", t=PACK))
+            nc.gpsimd.tensor_copy(dealt[:], raw[:].rearrange("p (m t) -> p t m", t=PACK))
 
         def gather(t, picked):
             nc.vector.tensor_copy(picked[:], y_rows[t][:].indirect(take_sb[:]))
@@ -139,35 +155,31 @@ def tile_picked_sharedexp_relu_po_kernel(
         def scatter(t, picked):
             nc.vector.tensor_tensor(z_rows[t][:].indirect(take_sb[:]), picked[:], wt_sb[:], MULT)
 
-        relu_y(0)
-        w4_codes = tile("w4_codes", [P, PACK, P], I32)
-        deal_words(w4_codes, w4_raw)
+        relu_y(first)
         picked0 = tile("picked0", [P, V], F32)
-        gather(0, picked0)
-        w34_scales = tile("w34_scales", [P, PACK, P], U8, "y_rows0")
-        nc.vector.tensor_copy(w34_scales[:], w34_raw_scales[:].rearrange("p (m t) -> p t m", t=PACK))
-        scatter(0, picked0)
+        gather(first, picked0)
+        scatter(first, picked0)
 
-        w2_bf = tile("w2_bf", [P, PACK, P, PACK], BF16)
+        w2_bf = placed_tile("w2_bf", [P, PACK, P, PACK], BF16, 6144)
         for u in range(2):
             nc.scalar.copy(
                 w2_bf[:].rearrange("p t m j -> p m j t")[:, u * 64 : (u + 1) * 64], w2_raw[u][:].rearrange("p j (m t) -> p m j t", t=PACK)
             )
-        for t in range(1, PACK):
+        for t in ORDER[1:]:
             relu_y(t)
         w2_codes, w2_scales = quantize("w2", w2_bf[:].rearrange("p t m j -> p (t m j)"), H)
         picked1 = tile("picked1", [P, V], F32)
         picked2 = tile("picked2", [P, V], F32)
-        gather(1, picked1)
-        gather(2, picked2)
-        scatter(1, picked1)
-        scatter(2, picked2)
-        w3_codes = tile("w3_codes", [P, PACK, P], I32, "picked2")
+        gather(second, picked1)
+        gather(third, picked2)
+        scatter(second, picked1)
+        scatter(third, picked2)
+        w4_codes = placed_tile("w4_codes", [P, PACK, P], I32, 6144)
+        deal_words(w4_codes, w4_raw)
+        w3_codes = placed_tile("w3_codes", [P, PACK, P], I32, 8192)
         deal_words(w3_codes, w3_raw)
 
         z2_bf = tile("z2_bf", [P, S, PACK], BF16)
-        zero_bias = tile("zero_bias", [P, 1], F32)
-        nc.vector.memset(zero_bias[:], 0.0)
         for c in range(S // CHUNK):
             acc = bank(c, [P, PACK, CHUNK])
             h, c0 = divmod(c * CHUNK, HALF)
@@ -181,21 +193,24 @@ def tile_picked_sharedexp_relu_po_kernel(
                     start=True,
                     stop=True,
                 )
-            nc.scalar.activation(z2_bf[:, c * CHUNK : (c + 1) * CHUNK, :], acc[:].rearrange("p t n -> p n t"), RELU, bias=zero_bias[:])
+            nc.scalar.activation(z2_bf[:, c * CHUNK : (c + 1) * CHUNK, :], acc[:].rearrange("p t n -> p n t"), RELU)
 
         z_bf = [tile("z_bf%d" % h, [P, HALF, PACK], BF16, ("w2_codes", "w2_scales")[h]) for h in range(2)]
 
-        def round_z(t, h):
-            copy = nc.vector.tensor_copy if t >= 2 and h == 0 else nc.scalar.copy
-            copy(z_bf[h][:, :, t], z_rows[t][:, h * HALF : (h + 1) * HALF])
+        def round_z(copy, t, h, n0=0, n1=HALF):
+            copy(z_bf[h][:, n0:n1, t], z_rows[t][:, h * HALF + n0 : h * HALF + n1])
 
-        for h in range(2):
-            for t in range(3):
-                round_z(t, h)
+        for t in ORDER[:-1]:
+            for h in range(2):
+                round_z(nc.scalar.copy, t, h)
 
-        picked3 = tile("picked3", [P, V], F32, "zero_bias")
+        w34_scales = placed_tile("w34_scales", [P, PACK, P], U8, 10240 + 1024)
+        deal_words(w34_scales, w34_raw_scales)
+        picked3 = placed_tile("picked3", [P, V], F32, 10240)
         gather(3, picked3)
-        z2_codes, z2_scales = quantize("z2", z2_bf[:].rearrange("p n t -> p (n t)"), S)
+        z2_codes = tile("z2_codes", [P, S], U32)
+        z2_scales = placed_tile("z2_scales", [P, S], U8, 10240 + 1536)
+        nc.vector.quantize_mx(out=z2_codes[:].bitcast(FP8X4), scales=z2_scales[:], in_=z2_bf[:].rearrange("p n t -> p (n t)"))
         out_acc = [[bank(PACK * (1 - h) + t, [P, HALF]) for t in range(PACK)] for h in range(2)]
         for h in range(2):
             for t in range(PACK):
@@ -209,8 +224,9 @@ def tile_picked_sharedexp_relu_po_kernel(
                     stop=False,
                 )
         scatter(3, picked3)
-        for h in range(2):
-            round_z(3, h)
+        round_z(nc.vector.tensor_copy, last, 0)
+        round_z(nc.vector.tensor_copy, last, 1, 0, CHUNK)
+        round_z(nc.scalar.copy, last, 1, CHUNK, HALF)
         for h in range(2):
             z_codes, z_scales = quantize("z%d" % h, z_bf[h][:].rearrange("p n t -> p (n t)"), HALF)
             for t in range(PACK):
@@ -248,16 +264,17 @@ def tile_picked_sharedexp_relu_po_kernel(
         for h in range(2):
             cols = slice(h * HALF, (h + 1) * HALF)
             for t in range(PACK):
-                copy = nc.vector.tensor_copy if h == 0 and t % 2 == 1 else nc.scalar.copy
+                copy = nc.vector.tensor_copy if (h, t) in ((0, 1), (0, 3), (1, 1)) else nc.scalar.copy
                 copy(out_f32[h][:, t, :], out_acc[h][t][:])
                 if t % 2 == 1:
                     nc.sync.dma_start(out_rows[:, t - 1 : t + 1, cols], out_f32[h][:, t - 1 : t + 1, :])
-        quantize_out(round_out(nc.vector.tensor_copy, 0, 0, HALF), 0, 0, HALF)
-        nc.sync.dma_start(out_words[:, :HALF], out_codes[0][:].bitcast(I32))
+        first_half = round_out(nc.vector.tensor_copy, 0, 0, HALF)
         by_vector = round_out(nc.vector.tensor_copy, 1, 0, CHUNK)
         by_scalar = round_out(nc.scalar.copy, 1, CHUNK, CHUNK)
-        quantize_out(by_scalar, 1, CHUNK, CHUNK)
+        quantize_out(first_half, 0, 0, HALF)
+        nc.sync.dma_start(out_words[:, :HALF], out_codes[0][:].bitcast(I32))
         quantize_out(by_vector, 1, 0, CHUNK)
+        quantize_out(by_scalar, 1, CHUNK, CHUNK)
         nc.sync.dma_start(out_words[:, HALF:], out_codes[1][:].bitcast(I32))
         for r in range(4):
             queue = nc.sync if r < 2 else nc.scalar

@@ -12,6 +12,7 @@ U16 = mybir.dt.uint16
 U8 = mybir.dt.uint8
 FP8X4 = mybir.dt.float8_e4m3fn_x4
 RELU = mybir.ActivationFunctionType.Relu
+IDENTITY = mybir.ActivationFunctionType.Identity
 MULT = mybir.AluOpType.mult
 
 P = 128
@@ -22,8 +23,8 @@ V = 256
 H = 512
 HALF = 256
 CHUNK = 128
-W1_VECTOR_M = 32
-ORDER = (2, 0, 1, 3)
+Z_VECTOR_COLS = 160
+ORDER = (0, 2, 3, 1)
 
 
 def as_words(packed):
@@ -39,8 +40,8 @@ def tile_picked_sharedexp_relu_po_kernel(
         placed = ctx.enter_context(tc.tile_pool(name="placed", bufs=1))
         psum = ctx.enter_context(tc.psum_pool(name="psum", bufs=1))
 
-        def tile(name, shape, dtype, after=None):
-            return sb.tile(shape, dtype, name=name, tag=after or name, align_bytes=64)
+        def tile(name, shape, dtype):
+            return sb.tile(shape, dtype, name=name, align_bytes=64)
 
         def placed_tile(name, shape, dtype, offset):
             return placed.tile(shape, dtype, name=name, align_bytes=64, offset=offset)
@@ -48,106 +49,105 @@ def tile_picked_sharedexp_relu_po_kernel(
         def bank(b, shape):
             return psum.tile(shape, F32, name="bank%d" % b, tag="bank%d" % b)
 
+        first, second, third, last = ORDER
+        at_w2a, at_w2b, at_w2_bf, at_w2_codes, at_z_second = 0, 4096, 9216, 13312, 15360
+
         offs_sb = tile("offs_sb", [P, S // 16], U16)
         take_sb = tile("take_sb", [P, V // 16], U16)
         x_table = tile("x_table", [P, T], U32)
         x_table_scales = tile("x_table_scales", [P, T], U8)
-        w1_raw = tile("w1_raw", [P, PACK, H], F32)
-        w2_raw = [tile("w2_raw0", [P, PACK, HALF], F32), placed_tile("w2_raw1", [P, PACK, HALF], F32, 1024)]
+        w1_raw = [tile("w1_raw%d" % i, [P, 2, H], F32) for i in range(2)]
+        w2_raw = [placed_tile("w2_raw0", [P, PACK, HALF], F32, at_w2a), placed_tile("w2_raw1", [P, PACK, HALF], F32, at_w2b)]
         wt_sb = tile("wt_sb", [P, V], F32)
         w3_raw = tile("w3_raw", [P, H], I32)
         w4_raw = tile("w4_raw", [P, H], I32)
         w34_raw_scales = tile("w34_raw_scales", [P, H], U8)
-        z_rows = [placed_tile("z_rows2", [P, S], F32, 10240) if t == 2 else tile("z_rows%d" % t, [P, S], F32) for t in range(PACK)]
+        z_rows = [placed_tile("z_rows_second", [P, S], F32, at_z_second) if t == second else tile("z_rows%d" % t, [P, S], F32) for t in range(PACK)]
 
         nc.vector.memset(x_table_scales[:].bitcast(I32), 0)
         nc.vector.memset(w34_raw_scales[:].bitcast(I32), 0)
         for t in range(PACK):
             nc.vector.memset(z_rows[t][:], 0.0)
 
-        def load_scales(plane, first, scales):
+        def load_scales(plane, row, scales):
             for r in range(4):
-                nc.sync.dma_start(plane[first + r : P : 32, :].bitcast(I32), scales[0, r:16:4, :].bitcast(I32))
+                nc.sync.dma_start(plane[row + r : P : 32, :].bitcast(I32), scales[0, r:16:4, :].bitcast(I32))
 
         def load_w2(u):
             nc.sync.dma_start(w2_raw[u][:], w2.rearrange("(p j) c -> p j c", j=PACK)[:, :, u * HALF : (u + 1) * HALF])
 
         nc.sync.dma_start(offs_sb[:], offs)
-        nc.sync.dma_start(take_sb[:], take)
-        nc.sync.dma_start(w1_raw[:], w1.rearrange("(p j) c -> p j c", j=PACK))
+        w1_by_rows = w1.rearrange("(p j) c -> p j c", j=PACK)
+        nc.sync.dma_start(w1_raw[0][:], w1_by_rows[:, :2])
         load_scales(x_table_scales, 0, x_scales)
+        nc.sync.dma_start(w1_raw[1][:], w1_by_rows[:, 2:])
         nc.sync.dma_start(x_table[:].bitcast(I32), as_words(x_words))
         load_w2(0)
-        nc.sync.dma_start(wt_sb[:], wt.rearrange("(p j) v -> p j v", j=PACK)[:, 0, :])
-        load_w2(1)
+        nc.sync.dma_start(take_sb[:], take)
         nc.sync.dma_start(w4_raw[:], as_words(w4_words))
         nc.sync.dma_start(w3_raw[:], as_words(w3_words))
+        nc.sync.dma_start(wt_sb[:], wt.rearrange("(p j) v -> p j v", j=PACK)[:, 0, :])
+        load_w2(1)
         load_scales(w34_raw_scales, 4, w4_scales)
         load_scales(w34_raw_scales, 0, w3_scales)
 
-        def deal_view(dealt, raw, ms):
+        def deal_view(dealt, raw, ms, m0=0):
             return (
-                dealt[:].rearrange("p t m j -> p m j t")[:, ms],
+                dealt[:].rearrange("p t m j -> p m j t")[:, m0 + ms.start : m0 + ms.stop],
                 raw[:].rearrange("p j (m t) -> p m j t", t=PACK)[:, ms],
             )
 
-        def quantize(name, grouped, cols):
-            codes = tile(name + "_codes", [P, cols], U32)
-            scales = tile(name + "_scales", [P, cols], U8)
-            nc.vector.quantize_mx(out=codes[:].bitcast(FP8X4), scales=scales[:], in_=grouped)
-            return codes, scales
+        def quantize(codes, scales, grouped):
+            nc.vector.quantize_mx(out=codes.bitcast(FP8X4), scales=scales, in_=grouped)
+
+        w1_bf = tile("w1_bf", [P, 2, 2, P, PACK], BF16)
+
+        def w1_views(u, js):
+            return (
+                w1_bf[:, u].rearrange("p v m j -> p m j v")[:, :, js],
+                w1_raw[js.start // 2][:].rearrange("p j (m v u) -> p u m j v", v=2, u=2)[:, u],
+            )
+
+        nc.scalar.copy(*w1_views(0, slice(0, 2)))
+        nc.scalar.copy(*w1_views(0, slice(2, 4)))
 
         xg_scales = tile("xg_scales", [P, S], U8)
         nc.vector.tensor_copy(xg_scales[:], x_table_scales[:].indirect(offs_sb[:]))
+        nc.vector.tensor_copy(*w1_views(1, slice(0, 2)))
+        nc.vector.tensor_copy(*w1_views(1, slice(2, 4)))
 
-        w1_bf = tile("w1_bf", [P, PACK, P, PACK], BF16)
-        nc.vector.tensor_copy(*deal_view(w1_bf, w1_raw, slice(0, W1_VECTOR_M)))
-        nc.scalar.copy(*deal_view(w1_bf, w1_raw, slice(W1_VECTOR_M, P)))
         w1_codes = tile("w1_codes", [P, H], U32)
         w1_scales = tile("w1_scales", [P, H], U8)
-
-        def quantize_w1(t0, t1):
-            nc.vector.quantize_mx(
-                out=w1_codes[:, t0 * P : t1 * P].bitcast(FP8X4),
-                scales=w1_scales[:, t0 * P : t1 * P],
-                in_=w1_bf[:, t0:t1].rearrange("p t m j -> p (t m j)"),
-            )
-
-        quantize_w1(2, 3)
+        for u in range(2):
+            quantize(w1_codes[:, u * HALF : (u + 1) * HALF], w1_scales[:, u * HALF : (u + 1) * HALF], w1_bf[:, u].rearrange("p v m j -> p (v m j)"))
 
         xg = [tile("xg%d" % h, [P, HALF], U32) for h in range(2)]
         for h in range(2):
             nc.vector.tensor_copy(xg[h][:], x_table[:].indirect(offs_sb[:, h * 16 : (h + 1) * 16]))
-        quantize_w1(0, 2)
-        quantize_w1(3, 4)
 
-        first, second, third, last = ORDER
-        y_rows = {first: tile("y_rows_first", [P, S], F32)}
-        for i, t in enumerate(ORDER[1:]):
-            y_rows[t] = placed_tile("y_rows%d" % t, [P, S], F32, 2048 * i)
-        y_acc = {t: [bank(2 * i + h, [P, HALF]) for h in range(2)] for i, t in enumerate(ORDER)}
-        for t in ORDER:
-            for h in range(2):
-                nc.tensor.matmul_mx(
-                    y_acc[t][h][:],
-                    lhsT=w1_codes[:, t * P : (t + 1) * P].bitcast(FP8X4),
-                    lhsT_scale=w1_scales[:, t * P : (t + 1) * P],
-                    rhs=xg[h][:].bitcast(FP8X4),
-                    rhs_scale=xg_scales[:, h * HALF : (h + 1) * HALF],
-                    start=True,
-                    stop=True,
-                )
-
-        def relu_y(t):
-            for h in range(2):
-                rows = y_rows[t][:, h * HALF : (h + 1) * HALF]
-                if t == first:
-                    nc.vector.tensor_scalar_max(rows, y_acc[t][h][:], 0.0)
-                else:
-                    nc.scalar.activation(rows, y_acc[t][h][:], RELU)
+        y_rows = {t: tile("y_rows%d" % t, [P, S], F32) for t in ORDER}
+        y_order = [(first, 0), (second, 0), (first, 1), (second, 1), (third, 0), (third, 1), (last, 0), (last, 1)]
+        for b, (t, h) in enumerate(y_order):
+            acc = bank(b % PACK, [P, HALF])
+            at = (2 * (t % 2) + t // 2) * P
+            nc.tensor.matmul_mx(
+                acc[:],
+                lhsT=w1_codes[:, at : at + P].bitcast(FP8X4),
+                lhsT_scale=w1_scales[:, at : at + P],
+                rhs=xg[h][:].bitcast(FP8X4),
+                rhs_scale=xg_scales[:, h * HALF : (h + 1) * HALF],
+                start=True,
+                stop=True,
+            )
+            nc.scalar.activation(y_rows[t][:, h * HALF : (h + 1) * HALF], acc[:], RELU)
 
         def deal_words(dealt, raw):
             nc.gpsimd.tensor_copy(dealt[:], raw[:].rearrange("p (m t) -> p t m", t=PACK))
+
+        w4_codes = tile("w4_codes", [P, PACK, P], I32)
+        deal_words(w4_codes, w4_raw)
+        w3_codes = tile("w3_codes", [P, PACK, P], I32)
+        deal_words(w3_codes, w3_raw)
 
         def gather(t, picked):
             nc.vector.tensor_copy(picked[:], y_rows[t][:].indirect(take_sb[:]))
@@ -155,33 +155,42 @@ def tile_picked_sharedexp_relu_po_kernel(
         def scatter(t, picked):
             nc.vector.tensor_tensor(z_rows[t][:].indirect(take_sb[:]), picked[:], wt_sb[:], MULT)
 
-        relu_y(first)
-        picked0 = tile("picked0", [P, V], F32)
-        gather(first, picked0)
-        scatter(first, picked0)
+        w2_bf = placed_tile("w2_bf", [P, PACK, P, PACK], BF16, at_w2_bf)
+        nc.vector.tensor_copy(*deal_view(w2_bf, w2_raw[0], slice(0, 64)))
 
-        w2_bf = placed_tile("w2_bf", [P, PACK, P, PACK], BF16, 6144)
-        for u in range(2):
-            nc.scalar.copy(
-                w2_bf[:].rearrange("p t m j -> p m j t")[:, u * 64 : (u + 1) * 64], w2_raw[u][:].rearrange("p j (m t) -> p m j t", t=PACK)
-            )
-        for t in ORDER[1:]:
-            relu_y(t)
-        w2_codes, w2_scales = quantize("w2", w2_bf[:].rearrange("p t m j -> p (t m j)"), H)
-        picked1 = tile("picked1", [P, V], F32)
-        picked2 = tile("picked2", [P, V], F32)
-        gather(second, picked1)
-        gather(third, picked2)
-        scatter(second, picked1)
-        scatter(third, picked2)
-        w4_codes = placed_tile("w4_codes", [P, PACK, P], I32, 6144)
-        deal_words(w4_codes, w4_raw)
-        w3_codes = placed_tile("w3_codes", [P, PACK, P], I32, 8192)
-        deal_words(w3_codes, w3_raw)
+        picked = {
+            first: placed_tile("picked_first", [P, V], F32, at_w2a),
+            second: placed_tile("picked_second", [P, V], F32, at_w2a + 1024),
+            third: placed_tile("picked_third", [P, V], F32, at_w2b),
+            last: placed_tile("picked_last", [P, V], F32, at_z_second),
+        }
+        gather(first, picked[first])
+        gather(second, picked[second])
+        scatter(first, picked[first])
 
-        z2_bf = tile("z2_bf", [P, S, PACK], BF16)
+        nc.scalar.activation(*deal_view(w2_bf, w2_raw[1], slice(0, 64), 64), IDENTITY, bias=z_rows[second][:, 0:1])
+        w2_codes = placed_tile("w2_codes", [P, H], U32, at_w2_codes)
+        w2_scales = tile("w2_scales", [P, H], U8)
+        quantize(w2_codes[:], w2_scales[:], w2_bf[:].rearrange("p t m j -> p (t m j)"))
+        gather(third, picked[third])
+        scatter(second, picked[second])
+        scatter(third, picked[third])
+        w34_scales = placed_tile("w34_scales", [P, PACK, P], U8, at_w2_bf)
+        deal_words(w34_scales, w34_raw_scales)
+
+        z_bf = [placed_tile("z_bf%d" % h, [P, HALF, PACK], BF16, at_w2b + 1024 + 2048 * h) for h in range(2)]
+
+        def round_z(copy, t, h, n0=0, n1=HALF):
+            copy(z_bf[h][:, n0:n1, t], z_rows[t][:, h * HALF + n0 : h * HALF + n1])
+
+        for h in range(2):
+            round_z(nc.scalar.copy, first, h)
+
+        z2_bf = [tile("z2_bf%d" % h, [P, HALF, PACK], BF16) for h in range(2)]
+        z_pair = placed_tile("z_pair", [P, 2, S], BF16, at_w2_codes)
+        z2_acc = []
         for c in range(S // CHUNK):
-            acc = bank(c, [P, PACK, CHUNK])
+            acc = bank(PACK + c, [P, PACK, CHUNK])
             h, c0 = divmod(c * CHUNK, HALF)
             for t in range(PACK):
                 nc.tensor.matmul_mx(
@@ -193,42 +202,49 @@ def tile_picked_sharedexp_relu_po_kernel(
                     start=True,
                     stop=True,
                 )
-            nc.scalar.activation(z2_bf[:, c * CHUNK : (c + 1) * CHUNK, :], acc[:].rearrange("p t n -> p n t"), RELU)
+            z2_acc.append(acc)
 
-        z_bf = [tile("z_bf%d" % h, [P, HALF, PACK], BF16, ("w2_codes", "w2_scales")[h]) for h in range(2)]
+        def relu_z2(c):
+            h, c0 = divmod(c * CHUNK, HALF)
+            nc.scalar.activation(z2_bf[h][:, c0 : c0 + CHUNK, :], z2_acc[c][:].rearrange("p t n -> p n t"), RELU)
 
-        def round_z(copy, t, h, n0=0, n1=HALF):
-            copy(z_bf[h][:, n0:n1, t], z_rows[t][:, h * HALF + n0 : h * HALF + n1])
-
-        for t in ORDER[:-1]:
-            for h in range(2):
-                round_z(nc.scalar.copy, t, h)
-
-        w34_scales = placed_tile("w34_scales", [P, PACK, P], U8, 10240 + 1024)
-        deal_words(w34_scales, w34_raw_scales)
-        picked3 = placed_tile("picked3", [P, V], F32, 10240)
-        gather(3, picked3)
-        z2_codes = tile("z2_codes", [P, S], U32)
-        z2_scales = placed_tile("z2_scales", [P, S], U8, 10240 + 1536)
-        nc.vector.quantize_mx(out=z2_codes[:].bitcast(FP8X4), scales=z2_scales[:], in_=z2_bf[:].rearrange("p n t -> p (n t)"))
-        out_acc = [[bank(PACK * (1 - h) + t, [P, HALF]) for t in range(PACK)] for h in range(2)]
+        for c in range(3):
+            relu_z2(c)
+        nc.scalar.copy(z_pair[:, 0, :], z_rows[second][:])
+        relu_z2(3)
         for h in range(2):
+            nc.scalar.copy(z_pair[:, 1, h * HALF : (h + 1) * HALF], z_rows[third][:, h * HALF : (h + 1) * HALF])
+        for h in range(2):
+            nc.scalar.copy(z_bf[h][:, :, second : third + 1], z_pair[:, :, h * HALF : (h + 1) * HALF].rearrange("p t n -> p n t"))
+
+        z2_codes = [tile("z2_codes%d" % h, [P, HALF], U32) for h in range(2)]
+        z2_scales = [placed_tile("z2_scales%d" % h, [P, HALF], U8, at_z_second + 1024 + 256 * h) for h in range(2)]
+        out_acc = [[bank(PACK * h + t, [P, HALF]) for t in range(PACK)] for h in range(2)]
+
+        def shared_passes(h):
+            quantize(z2_codes[h][:], z2_scales[h][:], z2_bf[h][:].rearrange("p n t -> p (n t)"))
             for t in range(PACK):
                 nc.tensor.matmul_mx(
                     out_acc[h][t][:],
                     lhsT=w4_codes[:, t, :].bitcast(FP8X4),
                     lhsT_scale=w34_scales[4:P, t, :],
-                    rhs=z2_codes[:, h * HALF : (h + 1) * HALF].bitcast(FP8X4),
-                    rhs_scale=z2_scales[:, h * HALF : (h + 1) * HALF],
+                    rhs=z2_codes[h][:].bitcast(FP8X4),
+                    rhs_scale=z2_scales[h][:],
                     start=True,
                     stop=False,
                 )
-        scatter(3, picked3)
-        round_z(nc.vector.tensor_copy, last, 0)
-        round_z(nc.vector.tensor_copy, last, 1, 0, CHUNK)
-        round_z(nc.scalar.copy, last, 1, CHUNK, HALF)
+
+        gather(last, picked[last])
+        shared_passes(0)
+        scatter(last, picked[last])
+        shared_passes(1)
         for h in range(2):
-            z_codes, z_scales = quantize("z%d" % h, z_bf[h][:].rearrange("p n t -> p (n t)"), HALF)
+            round_z(nc.vector.tensor_copy, last, h, 0, Z_VECTOR_COLS)
+            round_z(nc.scalar.copy, last, h, Z_VECTOR_COLS, HALF)
+        for h in range(2):
+            z_codes = tile("z_codes%d" % h, [P, HALF], U32)
+            z_scales = tile("z_scales%d" % h, [P, HALF], U8)
+            quantize(z_codes[:], z_scales[:], z_bf[h][:].rearrange("p n t -> p (n t)"))
             for t in range(PACK):
                 nc.tensor.matmul_mx(
                     out_acc[h][t][:],
@@ -246,19 +262,19 @@ def tile_picked_sharedexp_relu_po_kernel(
         out_f32 = [tile("out_f32_%d" % h, [P, PACK, HALF], F32) for h in range(2)]
         out_codes = [tile("out_codes%d" % h, [P, HALF], U32) for h in range(2)]
 
-        def round_out(copy, h, first, count):
-            rounded = tile("out_bf%d_%d" % (h, first), [P, count, PACK], BF16)
+        def round_out(copy, h, n0, count):
+            rounded = tile("out_bf%d_%d" % (h, n0), [P, count, PACK], BF16)
             copy(
                 rounded[:].rearrange("p (c i) t -> p c t i", i=4),
-                out_f32[h][:, :, first : first + count].rearrange("p t (c i) -> p c t i", i=4),
+                out_f32[h][:, :, n0 : n0 + count].rearrange("p t (c i) -> p c t i", i=4),
             )
             return rounded
 
-        def quantize_out(rounded, h, first, count):
-            nc.vector.quantize_mx(
-                out=out_codes[h][:, first : first + count].bitcast(FP8X4),
-                scales=out_scales[:, h * HALF + first : h * HALF + first + count],
-                in_=rounded[:].rearrange("p n t -> p (n t)"),
+        def quantize_out(rounded, h, n0, count):
+            quantize(
+                out_codes[h][:, n0 : n0 + count],
+                out_scales[:, h * HALF + n0 : h * HALF + n0 + count],
+                rounded[:].rearrange("p n t -> p (n t)"),
             )
 
         for h in range(2):
@@ -266,8 +282,9 @@ def tile_picked_sharedexp_relu_po_kernel(
             for t in range(PACK):
                 copy = nc.vector.tensor_copy if (h, t) in ((0, 1), (0, 3), (1, 1)) else nc.scalar.copy
                 copy(out_f32[h][:, t, :], out_acc[h][t][:])
-                if t % 2 == 1:
+                if h == 0 and t % 2 == 1:
                     nc.sync.dma_start(out_rows[:, t - 1 : t + 1, cols], out_f32[h][:, t - 1 : t + 1, :])
+        nc.sync.dma_start(out_rows[:, :, HALF:], out_f32[1][:])
         first_half = round_out(nc.vector.tensor_copy, 0, 0, HALF)
         by_vector = round_out(nc.vector.tensor_copy, 1, 0, CHUNK)
         by_scalar = round_out(nc.scalar.copy, 1, CHUNK, CHUNK)

@@ -22,6 +22,7 @@ S = 512
 V = 256
 H = 512
 HALF = 256
+W2_VECTOR_M = 48
 CHUNK = 128
 Z_VECTOR_COLS = 160
 ORDER = (0, 2, 3, 1)
@@ -50,16 +51,19 @@ def tile_picked_sharedexp_relu_po_kernel(
             return psum.tile(shape, F32, name="bank%d" % b, tag="bank%d" % b)
 
         first, second, third, last = ORDER
-        at_w2a, at_w2b, at_w2_bf, at_w2_codes, at_z_second = 0, 4096, 9216, 13312, 15360
+        at_w2a, at_w2b, at_w2_bf, at_w2_codes, at_z_second = 0, 4096, 9280, 13376, 15424
+
+        at_w3_raw = at_z_second + 2048
 
         offs_sb = tile("offs_sb", [P, S // 16], U16)
         take_sb = tile("take_sb", [P, V // 16], U16)
         x_table = tile("x_table", [P, T], U32)
         x_table_scales = tile("x_table_scales", [P, T], U8)
         w1_raw = [tile("w1_raw%d" % i, [P, 2, H], F32) for i in range(2)]
-        w2_raw = [placed_tile("w2_raw0", [P, PACK, HALF], F32, at_w2a), placed_tile("w2_raw1", [P, PACK, HALF], F32, at_w2b)]
+        w2_cols = (slice(0, PACK * W2_VECTOR_M), slice(PACK * W2_VECTOR_M, H))
+        w2_raw = [placed_tile("w2_raw%d" % u, [P, PACK, w2_cols[u].stop - w2_cols[u].start], F32, (at_w2a, at_w2b)[u]) for u in range(2)]
         wt_sb = tile("wt_sb", [P, V], F32)
-        w3_raw = tile("w3_raw", [P, H], I32)
+        w3_raw = placed_tile("w3_raw", [P, H], I32, at_w3_raw)
         w4_raw = tile("w4_raw", [P, H], I32)
         w34_raw_scales = tile("w34_raw_scales", [P, H], U8)
         z_rows = [placed_tile("z_rows_second", [P, S], F32, at_z_second) if t == second else tile("z_rows%d" % t, [P, S], F32) for t in range(PACK)]
@@ -74,7 +78,7 @@ def tile_picked_sharedexp_relu_po_kernel(
                 nc.sync.dma_start(plane[row + r : P : 32, :].bitcast(I32), scales[0, r:16:4, :].bitcast(I32))
 
         def load_w2(u):
-            nc.sync.dma_start(w2_raw[u][:], w2.rearrange("(p j) c -> p j c", j=PACK)[:, :, u * HALF : (u + 1) * HALF])
+            nc.sync.dma_start(w2_raw[u][:], w2.rearrange("(p j) c -> p j c", j=PACK)[:, :, w2_cols[u]])
 
         nc.sync.dma_start(offs_sb[:], offs)
         w1_by_rows = w1.rearrange("(p j) c -> p j c", j=PACK)
@@ -141,13 +145,10 @@ def tile_picked_sharedexp_relu_po_kernel(
             )
             nc.scalar.activation(y_rows[t][:, h * HALF : (h + 1) * HALF], acc[:], RELU)
 
-        def deal_words(dealt, raw):
-            nc.gpsimd.tensor_copy(dealt[:], raw[:].rearrange("p (m t) -> p t m", t=PACK))
-
-        w4_codes = tile("w4_codes", [P, PACK, P], I32)
-        deal_words(w4_codes, w4_raw)
-        w3_codes = tile("w3_codes", [P, PACK, P], I32)
-        deal_words(w3_codes, w3_raw)
+        def deal_packed(dealt, raw, run):
+            nc.vector.tensor_copy(
+                dealt[:].rearrange("p t (c i) -> p c t i", i=run), raw[:].rearrange("p (c i t) -> p c t i", i=run, t=PACK)
+            )
 
         def gather(t, picked):
             nc.vector.tensor_copy(picked[:], y_rows[t][:].indirect(take_sb[:]))
@@ -156,29 +157,33 @@ def tile_picked_sharedexp_relu_po_kernel(
             nc.vector.tensor_tensor(z_rows[t][:].indirect(take_sb[:]), picked[:], wt_sb[:], MULT)
 
         w2_bf = placed_tile("w2_bf", [P, PACK, P, PACK], BF16, at_w2_bf)
-        nc.vector.tensor_copy(*deal_view(w2_bf, w2_raw[0], slice(0, 64)))
+        nc.vector.tensor_copy(*deal_view(w2_bf, w2_raw[0], slice(0, W2_VECTOR_M)))
+        w4_codes = tile("w4_codes", [P, PACK, P], I32)
+        deal_packed(w4_codes, w4_raw, 4)
+        w3_codes = tile("w3_codes", [P, PACK, P], I32)
+        deal_packed(w3_codes, w3_raw, 4)
 
         picked = {
-            first: placed_tile("picked_first", [P, V], F32, at_w2a),
-            second: placed_tile("picked_second", [P, V], F32, at_w2a + 1024),
-            third: placed_tile("picked_third", [P, V], F32, at_w2b),
+            first: placed_tile("picked_first", [P, V], F32, at_w3_raw),
+            second: placed_tile("picked_second", [P, V], F32, at_w3_raw + 1024),
+            third: placed_tile("picked_third", [P, V], F32, at_w2b + 64),
             last: placed_tile("picked_last", [P, V], F32, at_z_second),
         }
         gather(first, picked[first])
         gather(second, picked[second])
         scatter(first, picked[first])
 
-        nc.scalar.activation(*deal_view(w2_bf, w2_raw[1], slice(0, 64), 64), IDENTITY, bias=z_rows[second][:, 0:1])
+        nc.scalar.activation(*deal_view(w2_bf, w2_raw[1], slice(0, P - W2_VECTOR_M), W2_VECTOR_M), IDENTITY, bias=z_rows[second][:, 0:1])
         w2_codes = placed_tile("w2_codes", [P, H], U32, at_w2_codes)
         w2_scales = tile("w2_scales", [P, H], U8)
         quantize(w2_codes[:], w2_scales[:], w2_bf[:].rearrange("p t m j -> p (t m j)"))
+        w34_scales = placed_tile("w34_scales", [P, PACK, P], U8, at_w2b - 448)
+        deal_packed(w34_scales, w34_raw_scales, 16)
         gather(third, picked[third])
         scatter(second, picked[second])
         scatter(third, picked[third])
-        w34_scales = placed_tile("w34_scales", [P, PACK, P], U8, at_w2_bf)
-        deal_words(w34_scales, w34_raw_scales)
 
-        z_bf = [placed_tile("z_bf%d" % h, [P, HALF, PACK], BF16, at_w2b + 1024 + 2048 * h) for h in range(2)]
+        z_bf = [placed_tile("z_bf%d" % h, [P, HALF, PACK], BF16, at_w2b + 1088 + 2048 * h) for h in range(2)]
 
         def round_z(copy, t, h, n0=0, n1=HALF):
             copy(z_bf[h][:, n0:n1, t], z_rows[t][:, h * HALF + n0 : h * HALF + n1])

@@ -22,9 +22,7 @@ S = 512
 V = 256
 H = 512
 HALF = 256
-W2_VECTOR_M = 48
 CHUNK = 128
-Z_VECTOR_COLS = 160
 ORDER = (0, 2, 3, 1)
 
 
@@ -51,22 +49,19 @@ def tile_picked_sharedexp_relu_po_kernel(
             return psum.tile(shape, F32, name="bank%d" % b, tag="bank%d" % b)
 
         first, second, third, last = ORDER
-        at_w2a, at_w2b, at_w2_bf, at_w2_codes, at_z_second = 0, 4096, 9280, 13376, 15424
-
-        at_w3_raw = at_z_second + 2048
+        at_w2_raw, at_w2_codes, at_w3_raw = 0, 8192, 11264
 
         offs_sb = tile("offs_sb", [P, S // 16], U16)
         take_sb = tile("take_sb", [P, V // 16], U16)
         x_table = tile("x_table", [P, T], U32)
         x_table_scales = tile("x_table_scales", [P, T], U8)
         w1_raw = [tile("w1_raw%d" % i, [P, 2, H], F32) for i in range(2)]
-        w2_cols = (slice(0, PACK * W2_VECTOR_M), slice(PACK * W2_VECTOR_M, H))
-        w2_raw = [placed_tile("w2_raw%d" % u, [P, PACK, w2_cols[u].stop - w2_cols[u].start], F32, (at_w2a, at_w2b)[u]) for u in range(2)]
+        w2_raw = placed_tile("w2_raw", [P, PACK, H], F32, at_w2_raw)
         wt_sb = tile("wt_sb", [P, V], F32)
         w3_raw = placed_tile("w3_raw", [P, H], I32, at_w3_raw)
         w4_raw = tile("w4_raw", [P, H], I32)
         w34_raw_scales = tile("w34_raw_scales", [P, H], U8)
-        z_rows = [placed_tile("z_rows_second", [P, S], F32, at_z_second) if t == second else tile("z_rows%d" % t, [P, S], F32) for t in range(PACK)]
+        z_rows = [tile("z_rows%d" % t, [P, S], F32) for t in range(PACK)]
 
         nc.vector.memset(x_table_scales[:].bitcast(I32), 0)
         nc.vector.memset(w34_raw_scales[:].bitcast(I32), 0)
@@ -77,29 +72,19 @@ def tile_picked_sharedexp_relu_po_kernel(
             for r in range(4):
                 nc.sync.dma_start(plane[row + r : P : 32, :].bitcast(I32), scales[0, r:16:4, :].bitcast(I32))
 
-        def load_w2(u):
-            nc.sync.dma_start(w2_raw[u][:], w2.rearrange("(p j) c -> p j c", j=PACK)[:, :, w2_cols[u]])
-
         nc.sync.dma_start(offs_sb[:], offs)
         w1_by_rows = w1.rearrange("(p j) c -> p j c", j=PACK)
         nc.sync.dma_start(w1_raw[0][:], w1_by_rows[:, :2])
         load_scales(x_table_scales, 0, x_scales)
         nc.sync.dma_start(w1_raw[1][:], w1_by_rows[:, 2:])
         nc.sync.dma_start(x_table[:].bitcast(I32), as_words(x_words))
-        load_w2(0)
-        nc.sync.dma_start(take_sb[:], take)
         nc.sync.dma_start(w4_raw[:], as_words(w4_words))
         nc.sync.dma_start(w3_raw[:], as_words(w3_words))
+        nc.sync.dma_start(take_sb[:], take)
         nc.sync.dma_start(wt_sb[:], wt.rearrange("(p j) v -> p j v", j=PACK)[:, 0, :])
-        load_w2(1)
+        nc.sync.dma_start(w2_raw[:], w2.rearrange("(p j) c -> p j c", j=PACK))
         load_scales(w34_raw_scales, 4, w4_scales)
         load_scales(w34_raw_scales, 0, w3_scales)
-
-        def deal_view(dealt, raw, ms, m0=0):
-            return (
-                dealt[:].rearrange("p t m j -> p m j t")[:, m0 + ms.start : m0 + ms.stop],
-                raw[:].rearrange("p j (m t) -> p m j t", t=PACK)[:, ms],
-            )
 
         def quantize(codes, scales, grouped):
             nc.vector.quantize_mx(out=codes.bitcast(FP8X4), scales=scales, in_=grouped)
@@ -156,40 +141,46 @@ def tile_picked_sharedexp_relu_po_kernel(
         def scatter(t, picked):
             nc.vector.tensor_tensor(z_rows[t][:].indirect(take_sb[:]), picked[:], wt_sb[:], MULT)
 
-        w2_bf = placed_tile("w2_bf", [P, PACK, P, PACK], BF16, at_w2_bf)
-        nc.vector.tensor_copy(*deal_view(w2_bf, w2_raw[0], slice(0, W2_VECTOR_M)))
         w4_codes = tile("w4_codes", [P, PACK, P], I32)
         deal_packed(w4_codes, w4_raw, 4)
         w3_codes = tile("w3_codes", [P, PACK, P], I32)
         deal_packed(w3_codes, w3_raw, 4)
 
         picked = {
-            first: placed_tile("picked_first", [P, V], F32, at_w3_raw),
-            second: placed_tile("picked_second", [P, V], F32, at_w3_raw + 1024),
-            third: placed_tile("picked_third", [P, V], F32, at_w2b + 64),
-            last: placed_tile("picked_last", [P, V], F32, at_z_second),
+            first: placed_tile("picked_first", [P, V], F32, at_w3_raw - 960),
+            second: placed_tile("picked_second", [P, V], F32, at_w3_raw + 64),
+            third: placed_tile("picked_third", [P, V], F32, at_w3_raw + 1088),
+            last: tile("picked_last", [P, V], F32),
         }
         gather(first, picked[first])
         gather(second, picked[second])
         scatter(first, picked[first])
+        gather(third, picked[third])
+        gather(last, picked[last])
 
-        nc.scalar.activation(*deal_view(w2_bf, w2_raw[1], slice(0, P - W2_VECTOR_M), W2_VECTOR_M), IDENTITY, bias=z_rows[second][:, 0:1])
+        w2_bf = tile("w2_bf", [P, PACK, P, PACK], BF16)
+        nc.scalar.activation(
+            w2_bf[:].rearrange("p t m j -> p m j t"),
+            w2_raw[:].rearrange("p j (m t) -> p m j t", t=PACK),
+            IDENTITY,
+            bias=z_rows[second][:, 0:1],
+        )
         w2_codes = placed_tile("w2_codes", [P, H], U32, at_w2_codes)
         w2_scales = tile("w2_scales", [P, H], U8)
         quantize(w2_codes[:], w2_scales[:], w2_bf[:].rearrange("p t m j -> p (t m j)"))
-        w34_scales = placed_tile("w34_scales", [P, PACK, P], U8, at_w2b - 448)
+        w34_scales = placed_tile("w34_scales", [P, PACK, P], U8, at_w2_raw + 4096)
         deal_packed(w34_scales, w34_raw_scales, 16)
-        gather(third, picked[third])
         scatter(second, picked[second])
-        scatter(third, picked[third])
 
-        z_bf = [placed_tile("z_bf%d" % h, [P, HALF, PACK], BF16, at_w2b + 1088 + 2048 * h) for h in range(2)]
+        z_bf = [placed_tile("z_bf%d" % h, [P, HALF, PACK], BF16, at_w2_raw + 2048 * h) for h in range(2)]
 
         def round_z(copy, t, h, n0=0, n1=HALF):
             copy(z_bf[h][:, n0:n1, t], z_rows[t][:, h * HALF + n0 : h * HALF + n1])
 
-        for h in range(2):
-            round_z(nc.scalar.copy, first, h)
+        nc.scalar.activation(z_bf[0][:, :, first], z_rows[first][:, :HALF], IDENTITY, bias=z_rows[third][:, 0:1])
+        round_z(nc.scalar.copy, first, 1)
+
+        scatter(third, picked[third])
 
         z2_bf = [tile("z2_bf%d" % h, [P, HALF, PACK], BF16) for h in range(2)]
         z_pair = placed_tile("z_pair", [P, 2, S], BF16, at_w2_codes)
@@ -209,21 +200,21 @@ def tile_picked_sharedexp_relu_po_kernel(
                 )
             z2_acc.append(acc)
 
-        def relu_z2(c):
+        def relu_z2(c, bias):
             h, c0 = divmod(c * CHUNK, HALF)
-            nc.scalar.activation(z2_bf[h][:, c0 : c0 + CHUNK, :], z2_acc[c][:].rearrange("p t n -> p n t"), RELU)
+            nc.scalar.activation(z2_bf[h][:, c0 : c0 + CHUNK, :], z2_acc[c][:].rearrange("p t n -> p n t"), RELU, bias=bias)
 
         for c in range(3):
-            relu_z2(c)
+            relu_z2(c, 0.0)
+        relu_z2(3, z_rows[last][:, 0:1])
         nc.scalar.copy(z_pair[:, 0, :], z_rows[second][:])
-        relu_z2(3)
         for h in range(2):
             nc.scalar.copy(z_pair[:, 1, h * HALF : (h + 1) * HALF], z_rows[third][:, h * HALF : (h + 1) * HALF])
         for h in range(2):
             nc.scalar.copy(z_bf[h][:, :, second : third + 1], z_pair[:, :, h * HALF : (h + 1) * HALF].rearrange("p t n -> p n t"))
 
         z2_codes = [tile("z2_codes%d" % h, [P, HALF], U32) for h in range(2)]
-        z2_scales = [placed_tile("z2_scales%d" % h, [P, HALF], U8, at_z_second + 1024 + 256 * h) for h in range(2)]
+        z2_scales = [tile("z2_scales%d" % h, [P, HALF], U8) for h in range(2)]
         out_acc = [[bank(PACK * h + t, [P, HALF]) for t in range(PACK)] for h in range(2)]
 
         def shared_passes(h):
@@ -239,13 +230,12 @@ def tile_picked_sharedexp_relu_po_kernel(
                     stop=False,
                 )
 
-        gather(last, picked[last])
         shared_passes(0)
         scatter(last, picked[last])
         shared_passes(1)
-        for h in range(2):
-            round_z(nc.vector.tensor_copy, last, h, 0, Z_VECTOR_COLS)
-            round_z(nc.scalar.copy, last, h, Z_VECTOR_COLS, HALF)
+        round_z(nc.vector.tensor_copy, last, 0)
+        round_z(nc.vector.tensor_copy, last, 1, 0, CHUNK)
+        round_z(nc.scalar.copy, last, 1, CHUNK, HALF)
         for h in range(2):
             z_codes = tile("z_codes%d" % h, [P, HALF], U32)
             z_scales = tile("z_scales%d" % h, [P, HALF], U8)
@@ -264,20 +254,20 @@ def tile_picked_sharedexp_relu_po_kernel(
         out_rows = out_0.rearrange("(p t) n -> p t n", t=PACK)
         out_words = as_words(out_1)
         out_scales = tile("out_scales", [P, S], U8)
-        out_f32 = [tile("out_f32_%d" % h, [P, PACK, HALF], F32) for h in range(2)]
-        out_codes = [tile("out_codes%d" % h, [P, HALF], U32) for h in range(2)]
+        out_f32 = tile("out_f32", [P, PACK, S], F32)
+        out_codes = tile("out_codes", [P, S], U32)
 
         def round_out(copy, h, n0, count):
             rounded = tile("out_bf%d_%d" % (h, n0), [P, count, PACK], BF16)
             copy(
                 rounded[:].rearrange("p (c i) t -> p c t i", i=4),
-                out_f32[h][:, :, n0 : n0 + count].rearrange("p t (c i) -> p c t i", i=4),
+                out_f32[:, :, h * HALF + n0 : h * HALF + n0 + count].rearrange("p t (c i) -> p c t i", i=4),
             )
             return rounded
 
         def quantize_out(rounded, h, n0, count):
             quantize(
-                out_codes[h][:, n0 : n0 + count],
+                out_codes[:, h * HALF + n0 : h * HALF + n0 + count],
                 out_scales[:, h * HALF + n0 : h * HALF + n0 + count],
                 rounded[:].rearrange("p n t -> p (n t)"),
             )
@@ -286,18 +276,17 @@ def tile_picked_sharedexp_relu_po_kernel(
             cols = slice(h * HALF, (h + 1) * HALF)
             for t in range(PACK):
                 copy = nc.vector.tensor_copy if (h, t) in ((0, 1), (0, 3), (1, 1)) else nc.scalar.copy
-                copy(out_f32[h][:, t, :], out_acc[h][t][:])
-                if h == 0 and t % 2 == 1:
-                    nc.sync.dma_start(out_rows[:, t - 1 : t + 1, cols], out_f32[h][:, t - 1 : t + 1, :])
-        nc.sync.dma_start(out_rows[:, :, HALF:], out_f32[1][:])
+                copy(out_f32[:, t, cols], out_acc[h][t][:])
+                if t == 1:
+                    nc.sync.dma_start(out_rows[:, :2, cols], out_f32[:, :2, cols])
+        nc.sync.dma_start(out_rows[:, 2:, :], out_f32[:, 2:, :])
         first_half = round_out(nc.vector.tensor_copy, 0, 0, HALF)
         by_vector = round_out(nc.vector.tensor_copy, 1, 0, CHUNK)
         by_scalar = round_out(nc.scalar.copy, 1, CHUNK, CHUNK)
         quantize_out(first_half, 0, 0, HALF)
-        nc.sync.dma_start(out_words[:, :HALF], out_codes[0][:].bitcast(I32))
         quantize_out(by_vector, 1, 0, CHUNK)
         quantize_out(by_scalar, 1, CHUNK, CHUNK)
-        nc.sync.dma_start(out_words[:, HALF:], out_codes[1][:].bitcast(I32))
+        nc.sync.dma_start(out_words, out_codes[:].bitcast(I32))
         for r in range(4):
             queue = nc.sync if r < 2 else nc.scalar
             queue.dma_start(out_2[0, r:16:4, :].bitcast(I32), out_scales[r:P:32, :].bitcast(I32))

@@ -49,14 +49,14 @@ def tile_picked_sharedexp_relu_po_kernel(
             return psum.tile(shape, F32, name="bank%d" % b, tag="bank%d" % b)
 
         first, second, third, last = ORDER
-        at_w2_raw, at_w2_codes, at_w3_raw = 0, 8192, 11264
+        at_w2_raw, at_w2_codes, at_w3_raw = 512, 8192, 11264
 
         offs_sb = tile("offs_sb", [P, S // 16], U16)
         take_sb = tile("take_sb", [P, V // 16], U16)
         x_table = tile("x_table", [P, T], U32)
         x_table_scales = tile("x_table_scales", [P, T], U8)
         w1_raw = [tile("w1_raw%d" % i, [P, 2, H], F32) for i in range(2)]
-        w2_raw = placed_tile("w2_raw", [P, PACK, H], F32, at_w2_raw)
+        w2_raw = [tile("w2_raw0", [P, PACK, HALF], F32), placed_tile("w2_raw1", [P, PACK, HALF], F32, at_w2_raw)]
         wt_sb = tile("wt_sb", [P, V], F32)
         w3_raw = placed_tile("w3_raw", [P, H], I32, at_w3_raw)
         w4_raw = tile("w4_raw", [P, H], I32)
@@ -65,6 +65,8 @@ def tile_picked_sharedexp_relu_po_kernel(
 
         nc.vector.memset(x_table_scales[:].bitcast(I32), 0)
         nc.vector.memset(w34_raw_scales[:].bitcast(I32), 0)
+        w34_scales = tile("w34_scales", [P, H], U8)
+        nc.vector.memset(w34_scales[:].bitcast(I32), 0)
         for t in range(PACK):
             nc.vector.memset(z_rows[t][:], 0.0)
 
@@ -78,13 +80,14 @@ def tile_picked_sharedexp_relu_po_kernel(
         load_scales(x_table_scales, 0, x_scales)
         nc.sync.dma_start(w1_raw[1][:], w1_by_rows[:, 2:])
         nc.sync.dma_start(x_table[:].bitcast(I32), as_words(x_words))
+        nc.sync.dma_start(w34_raw_scales[:16, :].bitcast(I32), w3_scales[0].bitcast(I32))
+        nc.sync.dma_start(w34_raw_scales[16:32, :].bitcast(I32), w4_scales[0].bitcast(I32))
         nc.sync.dma_start(w4_raw[:], as_words(w4_words))
         nc.sync.dma_start(w3_raw[:], as_words(w3_words))
         nc.sync.dma_start(take_sb[:], take)
         nc.sync.dma_start(wt_sb[:], wt.rearrange("(p j) v -> p j v", j=PACK)[:, 0, :])
-        nc.sync.dma_start(w2_raw[:], w2.rearrange("(p j) c -> p j c", j=PACK))
-        load_scales(w34_raw_scales, 4, w4_scales)
-        load_scales(w34_raw_scales, 0, w3_scales)
+        for u in range(2):
+            nc.sync.dma_start(w2_raw[u][:], w2.rearrange("(p j) c -> p j c", j=PACK)[:, :, u * HALF : (u + 1) * HALF])
 
         def quantize(codes, scales, grouped):
             nc.vector.quantize_mx(out=codes.bitcast(FP8X4), scales=scales, in_=grouped)
@@ -114,8 +117,14 @@ def tile_picked_sharedexp_relu_po_kernel(
         for h in range(2):
             nc.vector.tensor_copy(xg[h][:], x_table[:].indirect(offs_sb[:, h * 16 : (h + 1) * 16]))
 
-        y_rows = {t: tile("y_rows%d" % t, [P, S], F32) for t in ORDER}
-        y_order = [(first, 0), (second, 0), (first, 1), (second, 1), (third, 0), (third, 1), (last, 0), (last, 1)]
+        y_rows = {t: tile("y_rows%d" % t, [P, S], F32) for t in ORDER[:-1]}
+        y_rows[last] = placed_tile("y_rows_last", [P, S], F32, at_w2_raw + 4032)
+        y_acc = {}
+        y_order = [(t, h) for t in ORDER for h in range(2)]
+
+        def relu_y(t, h):
+            nc.scalar.activation(y_rows[t][:, h * HALF : (h + 1) * HALF], y_acc[t, h][:], RELU)
+
         for b, (t, h) in enumerate(y_order):
             acc = bank(b % PACK, [P, HALF])
             at = (2 * (t % 2) + t // 2) * P
@@ -128,7 +137,9 @@ def tile_picked_sharedexp_relu_po_kernel(
                 start=True,
                 stop=True,
             )
-            nc.scalar.activation(y_rows[t][:, h * HALF : (h + 1) * HALF], acc[:], RELU)
+            y_acc[t, h] = acc
+            if t != last:
+                relu_y(t, h)
 
         def deal_packed(dealt, raw, run):
             nc.vector.tensor_copy(
@@ -141,6 +152,12 @@ def tile_picked_sharedexp_relu_po_kernel(
         def scatter(t, picked):
             nc.vector.tensor_tensor(z_rows[t][:].indirect(take_sb[:]), picked[:], wt_sb[:], MULT)
 
+        w34_dealt_scales = tile("w34_dealt_scales", [P, PACK, P], U8)
+        deal_packed(w34_dealt_scales, w34_raw_scales, 16)
+        dealt_rows = w34_dealt_scales[:].rearrange("p t m -> p (t m)").bitcast(I32)
+        for i in (1, 0):
+            for q in range(4):
+                nc.sync.dma_start(w34_scales[32 * q + 4 * i : 32 * q + 4 * i + 4, :].bitcast(I32), dealt_rows[16 * i + 4 * q : 16 * i + 4 * q + 4, :])
         w4_codes = tile("w4_codes", [P, PACK, P], I32)
         deal_packed(w4_codes, w4_raw, 4)
         w3_codes = tile("w3_codes", [P, PACK, P], I32)
@@ -156,23 +173,24 @@ def tile_picked_sharedexp_relu_po_kernel(
         gather(second, picked[second])
         scatter(first, picked[first])
         gather(third, picked[third])
-        gather(last, picked[last])
 
         w2_bf = tile("w2_bf", [P, PACK, P, PACK], BF16)
+        nc.scalar.copy(w2_bf[:].rearrange("p t m j -> p m j t")[:, :64], w2_raw[0][:].rearrange("p j (m t) -> p m j t", t=PACK))
         nc.scalar.activation(
-            w2_bf[:].rearrange("p t m j -> p m j t"),
-            w2_raw[:].rearrange("p j (m t) -> p m j t", t=PACK),
+            w2_bf[:].rearrange("p t m j -> p m j t")[:, 64:],
+            w2_raw[1][:].rearrange("p j (m t) -> p m j t", t=PACK),
             IDENTITY,
             bias=z_rows[second][:, 0:1],
         )
         w2_codes = placed_tile("w2_codes", [P, H], U32, at_w2_codes)
         w2_scales = tile("w2_scales", [P, H], U8)
         quantize(w2_codes[:], w2_scales[:], w2_bf[:].rearrange("p t m j -> p (t m j)"))
-        w34_scales = placed_tile("w34_scales", [P, PACK, P], U8, at_w2_raw + 4096)
-        deal_packed(w34_scales, w34_raw_scales, 16)
+        for h in range(2):
+            relu_y(last, h)
+        gather(last, picked[last])
         scatter(second, picked[second])
 
-        z_bf = [placed_tile("z_bf%d" % h, [P, HALF, PACK], BF16, at_w2_raw + 2048 * h) for h in range(2)]
+        z_bf = [placed_tile("z_bf%d" % h, [P, HALF, PACK], BF16, at_w2_raw - 64 + 2048 * h) for h in range(2)]
 
         def round_z(copy, t, h, n0=0, n1=HALF):
             copy(z_bf[h][:, n0:n1, t], z_rows[t][:, h * HALF + n0 : h * HALF + n1])
@@ -204,9 +222,8 @@ def tile_picked_sharedexp_relu_po_kernel(
             h, c0 = divmod(c * CHUNK, HALF)
             nc.scalar.activation(z2_bf[h][:, c0 : c0 + CHUNK, :], z2_acc[c][:].rearrange("p t n -> p n t"), RELU, bias=bias)
 
-        for c in range(3):
-            relu_z2(c, 0.0)
-        relu_z2(3, z_rows[last][:, 0:1])
+        for c in range(S // CHUNK):
+            relu_z2(c, z_rows[last][:, 0:1] if c == 2 else 0.0)
         nc.scalar.copy(z_pair[:, 0, :], z_rows[second][:])
         for h in range(2):
             nc.scalar.copy(z_pair[:, 1, h * HALF : (h + 1) * HALF], z_rows[third][:, h * HALF : (h + 1) * HALF])
@@ -223,7 +240,7 @@ def tile_picked_sharedexp_relu_po_kernel(
                 nc.tensor.matmul_mx(
                     out_acc[h][t][:],
                     lhsT=w4_codes[:, t, :].bitcast(FP8X4),
-                    lhsT_scale=w34_scales[4:P, t, :],
+                    lhsT_scale=w34_scales[4:P, t * P : (t + 1) * P],
                     rhs=z2_codes[h][:].bitcast(FP8X4),
                     rhs_scale=z2_scales[h][:],
                     start=True,
@@ -244,7 +261,7 @@ def tile_picked_sharedexp_relu_po_kernel(
                 nc.tensor.matmul_mx(
                     out_acc[h][t][:],
                     lhsT=w3_codes[:, t, :].bitcast(FP8X4),
-                    lhsT_scale=w34_scales[:, t, :],
+                    lhsT_scale=w34_scales[:, t * P : (t + 1) * P],
                     rhs=z_codes[:].bitcast(FP8X4),
                     rhs_scale=z_scales[:],
                     start=False,
@@ -277,7 +294,9 @@ def tile_picked_sharedexp_relu_po_kernel(
             for t in range(PACK):
                 copy = nc.vector.tensor_copy if (h, t) in ((0, 1), (0, 3), (1, 1)) else nc.scalar.copy
                 copy(out_f32[:, t, cols], out_acc[h][t][:])
-                if t == 1:
+                if h == 0 and t < 2:
+                    nc.sync.dma_start(out_rows[:, t, cols], out_f32[:, t, cols])
+                if h == 1 and t == 1:
                     nc.sync.dma_start(out_rows[:, :2, cols], out_f32[:, :2, cols])
         nc.sync.dma_start(out_rows[:, 2:, :], out_f32[:, 2:, :])
         first_half = round_out(nc.vector.tensor_copy, 0, 0, HALF)

@@ -58,8 +58,7 @@ def tile_picked_sharedexp_relu_po_kernel(
         w1_raw = [tile("w1_raw%d" % i, [P, 2, H], F32) for i in range(2)]
         w2_raw = [tile("w2_raw0", [P, PACK, HALF], F32), placed_tile("w2_raw1", [P, PACK, HALF], F32, at_w2_raw)]
         wt_sb = tile("wt_sb", [P, V], F32)
-        w3_raw = placed_tile("w3_raw", [P, H], I32, at_w3_raw)
-        w4_raw = tile("w4_raw", [P, H], I32)
+        w34_raw = placed_tile("w34_raw", [P, 2 * H], I32, at_w3_raw)
         w34_raw_scales = tile("w34_raw_scales", [P, H], U8)
         z_rows = [tile("z_rows%d" % t, [P, S], F32) for t in range(PACK)]
 
@@ -74,16 +73,16 @@ def tile_picked_sharedexp_relu_po_kernel(
             for r in range(4):
                 nc.sync.dma_start(plane[row + r : P : 32, :].bitcast(I32), scales[0, r:16:4, :].bitcast(I32))
 
-        nc.sync.dma_start(offs_sb[:], offs)
         w1_by_rows = w1.rearrange("(p j) c -> p j c", j=PACK)
         nc.sync.dma_start(w1_raw[0][:], w1_by_rows[:, :2])
+        nc.sync.dma_start(offs_sb[:], offs)
         load_scales(x_table_scales, 0, x_scales)
         nc.sync.dma_start(w1_raw[1][:], w1_by_rows[:, 2:])
         nc.sync.dma_start(x_table[:].bitcast(I32), as_words(x_words))
         nc.sync.dma_start(w34_raw_scales[:16, :].bitcast(I32), w3_scales[0].bitcast(I32))
         nc.sync.dma_start(w34_raw_scales[16:32, :].bitcast(I32), w4_scales[0].bitcast(I32))
-        nc.sync.dma_start(w4_raw[:], as_words(w4_words))
-        nc.sync.dma_start(w3_raw[:], as_words(w3_words))
+        nc.sync.dma_start(w34_raw[:, H:], as_words(w4_words))
+        nc.sync.dma_start(w34_raw[:, :H], as_words(w3_words))
         nc.sync.dma_start(take_sb[:], take)
         nc.sync.dma_start(wt_sb[:], wt.rearrange("(p j) v -> p j v", j=PACK)[:, 0, :])
         for u in range(2):
@@ -120,26 +119,28 @@ def tile_picked_sharedexp_relu_po_kernel(
         y_rows = {t: tile("y_rows%d" % t, [P, S], F32) for t in ORDER[:-1]}
         y_rows[last] = placed_tile("y_rows_last", [P, S], F32, at_w2_raw + 4032)
         y_acc = {}
-        y_order = [(t, h) for t in ORDER for h in range(2)]
+        y_order = [(first, 0, HALF), (first, HALF, CHUNK), (first, HALF + CHUNK, CHUNK)]
+        y_order.extend((t, n0, HALF) for t in ORDER[1:] for n0 in (0, HALF))
 
-        def relu_y(t, h):
-            nc.scalar.activation(y_rows[t][:, h * HALF : (h + 1) * HALF], y_acc[t, h][:], RELU)
+        def relu_y(t, n0, count):
+            nc.scalar.activation(y_rows[t][:, n0 : n0 + count], y_acc[t, n0][:], RELU)
 
-        for b, (t, h) in enumerate(y_order):
-            acc = bank(b % PACK, [P, HALF])
+        for b, (t, n0, count) in enumerate(y_order):
+            acc = bank(b % (PACK + 1), [P, count])
             at = (2 * (t % 2) + t // 2) * P
+            h, c0 = divmod(n0, HALF)
             nc.tensor.matmul_mx(
                 acc[:],
                 lhsT=w1_codes[:, at : at + P].bitcast(FP8X4),
                 lhsT_scale=w1_scales[:, at : at + P],
-                rhs=xg[h][:].bitcast(FP8X4),
-                rhs_scale=xg_scales[:, h * HALF : (h + 1) * HALF],
+                rhs=xg[h][:, c0 : c0 + count].bitcast(FP8X4),
+                rhs_scale=xg_scales[:, n0 : n0 + count],
                 start=True,
                 stop=True,
             )
-            y_acc[t, h] = acc
+            y_acc[t, n0] = acc
             if t != last:
-                relu_y(t, h)
+                relu_y(t, n0, count)
 
         def deal_packed(dealt, raw, run):
             nc.vector.tensor_copy(
@@ -158,10 +159,8 @@ def tile_picked_sharedexp_relu_po_kernel(
         for i in (1, 0):
             for q in range(4):
                 nc.sync.dma_start(w34_scales[32 * q + 4 * i : 32 * q + 4 * i + 4, :].bitcast(I32), dealt_rows[16 * i + 4 * q : 16 * i + 4 * q + 4, :])
-        w4_codes = tile("w4_codes", [P, PACK, P], I32)
-        deal_packed(w4_codes, w4_raw, 4)
-        w3_codes = tile("w3_codes", [P, PACK, P], I32)
-        deal_packed(w3_codes, w3_raw, 4)
+        w34_codes = tile("w34_codes", [P, PACK, 2 * P], I32)
+        deal_packed(w34_codes, w34_raw, 4)
 
         picked = {
             first: placed_tile("picked_first", [P, V], F32, at_w3_raw - 960),
@@ -186,7 +185,7 @@ def tile_picked_sharedexp_relu_po_kernel(
         w2_scales = tile("w2_scales", [P, H], U8)
         quantize(w2_codes[:], w2_scales[:], w2_bf[:].rearrange("p t m j -> p (t m j)"))
         for h in range(2):
-            relu_y(last, h)
+            relu_y(last, h * HALF, HALF)
         gather(last, picked[last])
         scatter(second, picked[second])
 
@@ -239,7 +238,7 @@ def tile_picked_sharedexp_relu_po_kernel(
             for t in range(PACK):
                 nc.tensor.matmul_mx(
                     out_acc[h][t][:],
-                    lhsT=w4_codes[:, t, :].bitcast(FP8X4),
+                    lhsT=w34_codes[:, t, P:].bitcast(FP8X4),
                     lhsT_scale=w34_scales[4:P, t * P : (t + 1) * P],
                     rhs=z2_codes[h][:].bitcast(FP8X4),
                     rhs_scale=z2_scales[h][:],
@@ -260,7 +259,7 @@ def tile_picked_sharedexp_relu_po_kernel(
             for t in range(PACK):
                 nc.tensor.matmul_mx(
                     out_acc[h][t][:],
-                    lhsT=w3_codes[:, t, :].bitcast(FP8X4),
+                    lhsT=w34_codes[:, t, :P].bitcast(FP8X4),
                     lhsT_scale=w34_scales[:, t * P : (t + 1) * P],
                     rhs=z_codes[:].bitcast(FP8X4),
                     rhs_scale=z_scales[:],
@@ -294,11 +293,9 @@ def tile_picked_sharedexp_relu_po_kernel(
             for t in range(PACK):
                 copy = nc.vector.tensor_copy if (h, t) in ((0, 1), (0, 3), (1, 1)) else nc.scalar.copy
                 copy(out_f32[:, t, cols], out_acc[h][t][:])
-                if h == 0 and t < 2:
-                    nc.sync.dma_start(out_rows[:, t, cols], out_f32[:, t, cols])
-                if h == 1 and t == 1:
-                    nc.sync.dma_start(out_rows[:, :2, cols], out_f32[:, :2, cols])
-        nc.sync.dma_start(out_rows[:, 2:, :], out_f32[:, 2:, :])
+                if h == 0 and t % 2 == 1:
+                    nc.sync.dma_start(out_rows[:, t - 1 : t + 1, cols], out_f32[:, t - 1 : t + 1, cols])
+        nc.sync.dma_start(out_rows[:, :, HALF:], out_f32[:, :, HALF:])
         first_half = round_out(nc.vector.tensor_copy, 0, 0, HALF)
         by_vector = round_out(nc.vector.tensor_copy, 1, 0, CHUNK)
         by_scalar = round_out(nc.scalar.copy, 1, CHUNK, CHUNK)

@@ -13,7 +13,9 @@ U8 = mybir.dt.uint8
 FP8X4 = mybir.dt.float8_e4m3fn_x4
 RELU = mybir.ActivationFunctionType.Relu
 IDENTITY = mybir.ActivationFunctionType.Identity
+COPY = mybir.ActivationFunctionType.Copy
 MULT = mybir.AluOpType.mult
+ADD = mybir.AluOpType.add
 
 P = 128
 PACK = 4
@@ -48,17 +50,23 @@ def tile_picked_sharedexp_relu_po_kernel(
         def bank(b, shape):
             return psum.tile(shape, F32, name="bank%d" % b, tag="bank%d" % b)
 
-        first, second, third, last = ORDER
-        at_w2_raw, at_w2_codes, at_w3_raw = 512, 8192, 11264
+        def quantize(codes, scales, grouped):
+            nc.vector.quantize_mx(out=codes.bitcast(FP8X4), scales=scales, in_=grouped)
+
+        def mx_pass(acc, codes, scales, moving, moving_scales, start, stop):
+            nc.tensor.matmul_mx(
+                acc, lhsT=codes.bitcast(FP8X4), lhsT_scale=scales, rhs=moving.bitcast(FP8X4), rhs_scale=moving_scales, start=start, stop=stop
+            )
 
         offs_sb = tile("offs_sb", [P, S // 16], U16)
         take_sb = tile("take_sb", [P, V // 16], U16)
         x_table = tile("x_table", [P, T], U32)
         x_table_scales = tile("x_table_scales", [P, T], U8)
         w1_raw = [tile("w1_raw%d" % i, [P, 2, H], F32) for i in range(2)]
-        w2_raw = [tile("w2_raw0", [P, PACK, HALF], F32), placed_tile("w2_raw1", [P, PACK, HALF], F32, at_w2_raw)]
+        w2_raw = [tile("w2_raw%d" % u, [P, PACK, HALF], F32) for u in range(2)]
+        first, second, third, last = ORDER
         wt_sb = tile("wt_sb", [P, V], F32)
-        w34_raw = placed_tile("w34_raw", [P, 2 * H], I32, at_w3_raw)
+        w34_raw = tile("w34_raw", [P, 2 * H], I32)
         w34_raw_scales = tile("w34_raw_scales", [P, H], U8)
         z_rows = [tile("z_rows%d" % t, [P, S], F32) for t in range(PACK)]
 
@@ -69,27 +77,22 @@ def tile_picked_sharedexp_relu_po_kernel(
         for t in range(PACK):
             nc.vector.memset(z_rows[t][:], 0.0)
 
-        def load_scales(plane, row, scales):
-            for r in range(4):
-                nc.sync.dma_start(plane[row + r : P : 32, :].bitcast(I32), scales[0, r:16:4, :].bitcast(I32))
-
         w1_by_rows = w1.rearrange("(p j) c -> p j c", j=PACK)
+        w2_by_rows = w2.rearrange("(p j) c -> p j c", j=PACK)
         nc.sync.dma_start(w1_raw[0][:], w1_by_rows[:, :2])
         nc.sync.dma_start(offs_sb[:], offs)
-        load_scales(x_table_scales, 0, x_scales)
+        for r in range(4):
+            nc.sync.dma_start(x_table_scales[r:P:32, :].bitcast(I32), x_scales[0, r:16:4, :].bitcast(I32))
         nc.sync.dma_start(w1_raw[1][:], w1_by_rows[:, 2:])
         nc.sync.dma_start(x_table[:].bitcast(I32), as_words(x_words))
         nc.sync.dma_start(w34_raw_scales[:16, :].bitcast(I32), w3_scales[0].bitcast(I32))
         nc.sync.dma_start(w34_raw_scales[16:32, :].bitcast(I32), w4_scales[0].bitcast(I32))
+        nc.sync.dma_start(take_sb[:], take)
+        for u in range(2):
+            nc.sync.dma_start(w2_raw[u][:], w2_by_rows[:, :, u * HALF : (u + 1) * HALF])
+        nc.sync.dma_start(wt_sb[:], wt.rearrange("(p j) v -> p j v", j=PACK)[:, 0, :])
         nc.sync.dma_start(w34_raw[:, H:], as_words(w4_words))
         nc.sync.dma_start(w34_raw[:, :H], as_words(w3_words))
-        nc.sync.dma_start(take_sb[:], take)
-        nc.sync.dma_start(wt_sb[:], wt.rearrange("(p j) v -> p j v", j=PACK)[:, 0, :])
-        for u in range(2):
-            nc.sync.dma_start(w2_raw[u][:], w2.rearrange("(p j) c -> p j c", j=PACK)[:, :, u * HALF : (u + 1) * HALF])
-
-        def quantize(codes, scales, grouped):
-            nc.vector.quantize_mx(out=codes.bitcast(FP8X4), scales=scales, in_=grouped)
 
         w1_bf = tile("w1_bf", [P, 2, 2, P, PACK], BF16)
 
@@ -99,13 +102,13 @@ def tile_picked_sharedexp_relu_po_kernel(
                 w1_raw[js.start // 2][:].rearrange("p j (m v u) -> p u m j v", v=2, u=2)[:, u],
             )
 
-        nc.scalar.copy(*w1_views(0, slice(0, 2)))
-        nc.scalar.copy(*w1_views(0, slice(2, 4)))
+        nc.scalar.copy(*w1_views(1, slice(0, 2)))
+        nc.scalar.copy(*w1_views(1, slice(2, 4)))
 
         xg_scales = tile("xg_scales", [P, S], U8)
         nc.vector.tensor_copy(xg_scales[:], x_table_scales[:].indirect(offs_sb[:]))
-        nc.vector.tensor_copy(*w1_views(1, slice(0, 2)))
-        nc.vector.tensor_copy(*w1_views(1, slice(2, 4)))
+        nc.vector.tensor_copy(*w1_views(0, slice(0, 2)))
+        nc.vector.tensor_copy(*w1_views(0, slice(2, 4)))
 
         w1_codes = tile("w1_codes", [P, H], U32)
         w1_scales = tile("w1_scales", [P, H], U8)
@@ -116,42 +119,28 @@ def tile_picked_sharedexp_relu_po_kernel(
         for h in range(2):
             nc.vector.tensor_copy(xg[h][:], x_table[:].indirect(offs_sb[:, h * 16 : (h + 1) * 16]))
 
-        y_rows = {t: tile("y_rows%d" % t, [P, S], F32) for t in ORDER[:-1]}
-        y_rows[last] = placed_tile("y_rows_last", [P, S], F32, at_w2_raw + 4032)
-        y_acc = {}
-        y_order = [(first, 0, HALF), (first, HALF, CHUNK), (first, HALF + CHUNK, CHUNK)]
-        y_order.extend((t, n0, HALF) for t in ORDER[1:] for n0 in (0, HALF))
-
-        def relu_y(t, n0, count):
-            nc.scalar.activation(y_rows[t][:, n0 : n0 + count], y_acc[t, n0][:], RELU)
-
-        for b, (t, n0, count) in enumerate(y_order):
-            acc = bank(b % (PACK + 1), [P, count])
+        picked = {}
+        banks_used = 0
+        for k, t in enumerate(ORDER):
+            y_rows = sb.tile([P, S], F32, name="y_rows", tag="y_rows", bufs=2, align_bytes=64)
             at = (2 * (t % 2) + t // 2) * P
-            h, c0 = divmod(n0, HALF)
-            nc.tensor.matmul_mx(
-                acc[:],
-                lhsT=w1_codes[:, at : at + P].bitcast(FP8X4),
-                lhsT_scale=w1_scales[:, at : at + P],
-                rhs=xg[h][:, c0 : c0 + count].bitcast(FP8X4),
-                rhs_scale=xg_scales[:, n0 : n0 + count],
-                start=True,
-                stop=True,
-            )
-            y_acc[t, n0] = acc
-            if t != last:
-                relu_y(t, n0, count)
+            pieces = [(0, HALF), (HALF, CHUNK), (HALF + CHUNK, CHUNK)] if k == 0 else [(0, HALF), (HALF, HALF)]
+            for n0, count in pieces:
+                acc = bank(banks_used % PACK, [P, count])
+                banks_used = banks_used + 1
+                h, c0 = divmod(n0, HALF)
+                mx_pass(acc[:], w1_codes[:, at : at + P], w1_scales[:, at : at + P], xg[h][:, c0 : c0 + count], xg_scales[:, n0 : n0 + count], True, True)
+                nc.scalar.activation(y_rows[:, n0 : n0 + count], acc[:], RELU)
+            picked[t] = tile("picked%d" % (first if t == third else t), [P, V], F32)
+            nc.scalar.activation(picked[t][:], y_rows[:].indirect(take_sb[:]), COPY)
 
         def deal_packed(dealt, raw, run):
             nc.vector.tensor_copy(
                 dealt[:].rearrange("p t (c i) -> p c t i", i=run), raw[:].rearrange("p (c i t) -> p c t i", i=run, t=PACK)
             )
 
-        def gather(t, picked):
-            nc.vector.tensor_copy(picked[:], y_rows[t][:].indirect(take_sb[:]))
-
-        def scatter(t, picked):
-            nc.vector.tensor_tensor(z_rows[t][:].indirect(take_sb[:]), picked[:], wt_sb[:], MULT)
+        def scatter(t):
+            nc.vector.tensor_tensor(z_rows[t][:].indirect(take_sb[:]), picked[t][:], wt_sb[:], MULT)
 
         w34_dealt_scales = tile("w34_dealt_scales", [P, PACK, P], U8)
         deal_packed(w34_dealt_scales, w34_raw_scales, 16)
@@ -159,113 +148,70 @@ def tile_picked_sharedexp_relu_po_kernel(
         for i in (1, 0):
             for q in range(4):
                 nc.sync.dma_start(w34_scales[32 * q + 4 * i : 32 * q + 4 * i + 4, :].bitcast(I32), dealt_rows[16 * i + 4 * q : 16 * i + 4 * q + 4, :])
-        w34_codes = tile("w34_codes", [P, PACK, 2 * P], I32)
-        deal_packed(w34_codes, w34_raw, 4)
-
-        picked = {
-            first: placed_tile("picked_first", [P, V], F32, at_w3_raw - 960),
-            second: placed_tile("picked_second", [P, V], F32, at_w3_raw + 64),
-            third: placed_tile("picked_third", [P, V], F32, at_w3_raw + 1088),
-            last: tile("picked_last", [P, V], F32),
-        }
-        gather(first, picked[first])
-        gather(second, picked[second])
-        scatter(first, picked[first])
-        gather(third, picked[third])
 
         w2_bf = tile("w2_bf", [P, PACK, P, PACK], BF16)
-        nc.scalar.copy(w2_bf[:].rearrange("p t m j -> p m j t")[:, :64], w2_raw[0][:].rearrange("p j (m t) -> p m j t", t=PACK))
-        nc.scalar.activation(
-            w2_bf[:].rearrange("p t m j -> p m j t")[:, 64:],
-            w2_raw[1][:].rearrange("p j (m t) -> p m j t", t=PACK),
-            IDENTITY,
-            bias=z_rows[second][:, 0:1],
-        )
-        w2_codes = placed_tile("w2_codes", [P, H], U32, at_w2_codes)
+        w2_views = [
+            (w2_bf[:].rearrange("p t m j -> p m j t")[:, 64 * u : 64 * (u + 1)], w2_raw[u][:].rearrange("p j (m t) -> p m j t", t=PACK))
+            for u in range(2)
+        ]
+        nc.vector.tensor_copy(*w2_views[0])
+        nc.vector.tensor_scalar(*w2_views[1], z_rows[first][:, 0:1], z_rows[second][:, 0:1], ADD, ADD)
+        w2_codes = placed_tile("w2_codes", [P, H], U32, 4096)
         w2_scales = tile("w2_scales", [P, H], U8)
         quantize(w2_codes[:], w2_scales[:], w2_bf[:].rearrange("p t m j -> p (t m j)"))
-        for h in range(2):
-            relu_y(last, h * HALF, HALF)
-        gather(last, picked[last])
-        scatter(second, picked[second])
-
-        z_bf = [placed_tile("z_bf%d" % h, [P, HALF, PACK], BF16, at_w2_raw - 64 + 2048 * h) for h in range(2)]
-
-        def round_z(copy, t, h, n0=0, n1=HALF):
-            copy(z_bf[h][:, n0:n1, t], z_rows[t][:, h * HALF + n0 : h * HALF + n1])
-
-        nc.scalar.activation(z_bf[0][:, :, first], z_rows[first][:, :HALF], IDENTITY, bias=z_rows[third][:, 0:1])
-        round_z(nc.scalar.copy, first, 1)
-
-        scatter(third, picked[third])
+        scatter(first)
+        scatter(second)
+        scatter(third)
 
         z2_bf = [tile("z2_bf%d" % h, [P, HALF, PACK], BF16) for h in range(2)]
-        z_pair = placed_tile("z_pair", [P, 2, S], BF16, at_w2_codes)
-        z2_acc = []
         for c in range(S // CHUNK):
             acc = bank(PACK + c, [P, PACK, CHUNK])
             h, c0 = divmod(c * CHUNK, HALF)
             for t in range(PACK):
-                nc.tensor.matmul_mx(
-                    acc[:, t, :],
-                    lhsT=w2_codes[:, t * P : (t + 1) * P].bitcast(FP8X4),
-                    lhsT_scale=w2_scales[:, t * P : (t + 1) * P],
-                    rhs=xg[h][:, c0 : c0 + CHUNK].bitcast(FP8X4),
-                    rhs_scale=xg_scales[:, c * CHUNK : (c + 1) * CHUNK],
-                    start=True,
-                    stop=True,
-                )
-            z2_acc.append(acc)
+                mx_pass(acc[:, t, :], w2_codes[:, t * P : (t + 1) * P], w2_scales[:, t * P : (t + 1) * P], xg[h][:, c0 : c0 + CHUNK], xg_scales[:, c * CHUNK : (c + 1) * CHUNK], True, True)
+            nc.scalar.activation(
+                z2_bf[h][:, c0 : c0 + CHUNK, :], acc[:].rearrange("p t n -> p n t"), RELU, bias=z_rows[last][:, 0:1] if c == 3 else 0.0
+            )
 
-        def relu_z2(c, bias):
-            h, c0 = divmod(c * CHUNK, HALF)
-            nc.scalar.activation(z2_bf[h][:, c0 : c0 + CHUNK, :], z2_acc[c][:].rearrange("p t n -> p n t"), RELU, bias=bias)
+        w34_codes = placed_tile("w34_codes", [P, 2, PACK, P], U32, 64)
+        z_pairs = placed_tile("z_pairs", [P, 2, S, 2], BF16, 4096 + 64)
 
-        for c in range(S // CHUNK):
-            relu_z2(c, z_rows[last][:, 0:1] if c == 2 else 0.0)
-        nc.scalar.copy(z_pair[:, 0, :], z_rows[second][:])
-        for h in range(2):
-            nc.scalar.copy(z_pair[:, 1, h * HALF : (h + 1) * HALF], z_rows[third][:, h * HALF : (h + 1) * HALF])
-        for h in range(2):
-            nc.scalar.copy(z_bf[h][:, :, second : third + 1], z_pair[:, :, h * HALF : (h + 1) * HALF].rearrange("p t n -> p n t"))
+        def deal_words(i):
+            nc.scalar.copy(
+                w34_codes[:, i].rearrange("p t (c k) -> p c t k", k=4),
+                w34_raw[:, i * H : (i + 1) * H].bitcast(U32).rearrange("p (c k t) -> p c t k", k=4, t=PACK),
+            )
 
-        z2_codes = [tile("z2_codes%d" % h, [P, HALF], U32) for h in range(2)]
-        z2_scales = [tile("z2_scales%d" % h, [P, HALF], U8) for h in range(2)]
+        nc.vector.tensor_copy(z_pairs[:, first // 2, :, first % 2], z_rows[first][:])
+        deal_words(1)
+        for t in (second, third):
+            nc.scalar.copy(z_pairs[:, t // 2, :, t % 2], z_rows[t][:])
+        deal_words(0)
+
         out_acc = [[bank(PACK * h + t, [P, HALF]) for t in range(PACK)] for h in range(2)]
-
-        def shared_passes(h):
-            quantize(z2_codes[h][:], z2_scales[h][:], z2_bf[h][:].rearrange("p n t -> p (n t)"))
+        for h in range(2):
+            z2_codes = tile("z2_codes%d" % h, [P, HALF], U32)
+            z2_scales = tile("z2_scales%d" % h, [P, HALF], U8)
+            quantize(z2_codes[:], z2_scales[:], z2_bf[h][:].rearrange("p n t -> p (n t)"))
             for t in range(PACK):
-                nc.tensor.matmul_mx(
-                    out_acc[h][t][:],
-                    lhsT=w34_codes[:, t, P:].bitcast(FP8X4),
-                    lhsT_scale=w34_scales[4:P, t * P : (t + 1) * P],
-                    rhs=z2_codes[h][:].bitcast(FP8X4),
-                    rhs_scale=z2_scales[h][:],
-                    start=True,
-                    stop=False,
-                )
+                mx_pass(out_acc[h][t][:], w34_codes[:, 1, t], w34_scales[4:P, t * P : (t + 1) * P], z2_codes[:], z2_scales[:], True, False)
+        scatter(last)
 
-        shared_passes(0)
-        scatter(last, picked[last])
-        shared_passes(1)
-        round_z(nc.vector.tensor_copy, last, 0)
-        round_z(nc.vector.tensor_copy, last, 1, 0, CHUNK)
-        round_z(nc.scalar.copy, last, 1, CHUNK, HALF)
+        z_bf = [tile("z_bf%d" % h, [P, HALF, PACK], BF16) for h in range(2)]
+        for h in range(2):
+            nc.vector.tensor_copy(z_pairs[:, last // 2, h * HALF : (h + 1) * HALF, last % 2], z_rows[last][:, h * HALF : (h + 1) * HALF])
+        pair_words = z_pairs[:].rearrange("p u n e -> p (u n e)").bitcast(F32).rearrange("p (u n) -> p u n", u=2)
+        for h, copy in enumerate((nc.vector.tensor_copy, nc.vector.tensor_copy)):
+            copy(
+                z_bf[h][:].rearrange("p n t -> p (n t)").bitcast(F32).rearrange("p (c i u) -> p c u i", i=4, u=2),
+                pair_words[:, :, h * HALF : (h + 1) * HALF].rearrange("p u (c i) -> p c u i", i=4),
+            )
         for h in range(2):
             z_codes = tile("z_codes%d" % h, [P, HALF], U32)
             z_scales = tile("z_scales%d" % h, [P, HALF], U8)
             quantize(z_codes[:], z_scales[:], z_bf[h][:].rearrange("p n t -> p (n t)"))
             for t in range(PACK):
-                nc.tensor.matmul_mx(
-                    out_acc[h][t][:],
-                    lhsT=w34_codes[:, t, :P].bitcast(FP8X4),
-                    lhsT_scale=w34_scales[:, t * P : (t + 1) * P],
-                    rhs=z_codes[:].bitcast(FP8X4),
-                    rhs_scale=z_scales[:],
-                    start=False,
-                    stop=True,
-                )
+                mx_pass(out_acc[h][t][:], w34_codes[:, 0, t], w34_scales[:, t * P : (t + 1) * P], z_codes[:], z_scales[:], False, True)
 
         out_rows = out_0.rearrange("(p t) n -> p t n", t=PACK)
         out_words = as_words(out_1)

@@ -131,7 +131,10 @@ def tile_picked_sharedexp_relu_po_kernel(
                 h, c0 = divmod(n0, HALF)
                 mx_pass(acc[:], w1_codes[:, at : at + P], w1_scales[:, at : at + P], xg[h][:, c0 : c0 + count], xg_scales[:, n0 : n0 + count], True, True)
                 nc.scalar.activation(y_rows[:, n0 : n0 + count], acc[:], RELU)
-            picked[t] = tile("picked%d" % (first if t == third else t), [P, V], F32)
+            if t == last:
+                picked[t] = placed_tile("picked_last", [P, V], F32, 0)
+            else:
+                picked[t] = tile("picked%d" % (first if t == third else t), [P, V], F32)
             nc.scalar.activation(picked[t][:], y_rows[:].indirect(take_sb[:]), COPY)
 
         def deal_packed(dealt, raw, run):
@@ -150,18 +153,27 @@ def tile_picked_sharedexp_relu_po_kernel(
                 nc.sync.dma_start(w34_scales[32 * q + 4 * i : 32 * q + 4 * i + 4, :].bitcast(I32), dealt_rows[16 * i + 4 * q : 16 * i + 4 * q + 4, :])
 
         w2_bf = tile("w2_bf", [P, PACK, P, PACK], BF16)
-        w2_views = [
-            (w2_bf[:].rearrange("p t m j -> p m j t")[:, 64 * u : 64 * (u + 1)], w2_raw[u][:].rearrange("p j (m t) -> p m j t", t=PACK))
-            for u in range(2)
-        ]
-        nc.vector.tensor_copy(*w2_views[0])
-        nc.vector.tensor_scalar(*w2_views[1], z_rows[first][:, 0:1], z_rows[second][:, 0:1], ADD, ADD)
+
+        def w2_views(u, ts):
+            return (
+                w2_bf[:].rearrange("p t m j -> p m j t")[:, 64 * u : 64 * (u + 1), :, ts],
+                w2_raw[u][:].rearrange("p j (m t) -> p m j t", t=PACK)[:, :, :, ts],
+            )
+
+        nc.vector.tensor_copy(*w2_views(0, slice(0, 4)))
+        nc.vector.tensor_scalar(*w2_views(1, slice(0, 4)), z_rows[first][:, 0:1], z_rows[second][:, 0:1], ADD, ADD)
         w2_codes = placed_tile("w2_codes", [P, H], U32, 4096)
         w2_scales = tile("w2_scales", [P, H], U8)
         quantize(w2_codes[:], w2_scales[:], w2_bf[:].rearrange("p t m j -> p (t m j)"))
         scatter(first)
         scatter(second)
         scatter(third)
+
+        def deal_words(codes, i):
+            nc.scalar.copy(
+                codes[:].rearrange("p t (c k) -> p c t k", k=4),
+                w34_raw[:, i * H : (i + 1) * H].bitcast(U32).rearrange("p (c k t) -> p c t k", k=4, t=PACK),
+            )
 
         z2_bf = [tile("z2_bf%d" % h, [P, HALF, PACK], BF16) for h in range(2)]
         for c in range(S // CHUNK):
@@ -173,29 +185,27 @@ def tile_picked_sharedexp_relu_po_kernel(
                 z2_bf[h][:, c0 : c0 + CHUNK, :], acc[:].rearrange("p t n -> p n t"), RELU, bias=z_rows[last][:, 0:1] if c == 3 else 0.0
             )
 
-        w34_codes = placed_tile("w34_codes", [P, 2, PACK, P], U32, 64)
+        w4_codes = placed_tile("w4_codes", [P, PACK, P], U32, 2048 + 64)
+        w3_codes = placed_tile("w3_codes", [P, PACK, P], U32, 0)
         z_pairs = placed_tile("z_pairs", [P, 2, S, 2], BF16, 4096 + 64)
-
-        def deal_words(i):
-            nc.scalar.copy(
-                w34_codes[:, i].rearrange("p t (c k) -> p c t k", k=4),
-                w34_raw[:, i * H : (i + 1) * H].bitcast(U32).rearrange("p (c k t) -> p c t k", k=4, t=PACK),
-            )
-
         nc.vector.tensor_copy(z_pairs[:, first // 2, :, first % 2], z_rows[first][:])
-        deal_words(1)
+        deal_words(w4_codes, 1)
         for t in (second, third):
             nc.scalar.copy(z_pairs[:, t // 2, :, t % 2], z_rows[t][:])
-        deal_words(0)
+        deal_words(w3_codes, 0)
 
         out_acc = [[bank(PACK * h + t, [P, HALF]) for t in range(PACK)] for h in range(2)]
-        for h in range(2):
+
+        def shared_passes(h):
             z2_codes = tile("z2_codes%d" % h, [P, HALF], U32)
             z2_scales = tile("z2_scales%d" % h, [P, HALF], U8)
             quantize(z2_codes[:], z2_scales[:], z2_bf[h][:].rearrange("p n t -> p (n t)"))
             for t in range(PACK):
-                mx_pass(out_acc[h][t][:], w34_codes[:, 1, t], w34_scales[4:P, t * P : (t + 1) * P], z2_codes[:], z2_scales[:], True, False)
+                mx_pass(out_acc[h][t][:], w4_codes[:, t], w34_scales[4:P, t * P : (t + 1) * P], z2_codes[:], z2_scales[:], True, False)
+
+        shared_passes(0)
         scatter(last)
+        shared_passes(1)
 
         z_bf = [tile("z_bf%d" % h, [P, HALF, PACK], BF16) for h in range(2)]
         for h in range(2):
@@ -211,7 +221,7 @@ def tile_picked_sharedexp_relu_po_kernel(
             z_scales = tile("z_scales%d" % h, [P, HALF], U8)
             quantize(z_codes[:], z_scales[:], z_bf[h][:].rearrange("p n t -> p (n t)"))
             for t in range(PACK):
-                mx_pass(out_acc[h][t][:], w34_codes[:, 0, t], w34_scales[:, t * P : (t + 1) * P], z_codes[:], z_scales[:], False, True)
+                mx_pass(out_acc[h][t][:], w3_codes[:, t], w34_scales[:, t * P : (t + 1) * P], z_codes[:], z_scales[:], False, True)
 
         out_rows = out_0.rearrange("(p t) n -> p t n", t=PACK)
         out_words = as_words(out_1)

@@ -25,7 +25,7 @@ V = 256
 H = 512
 HALF = 256
 CHUNK = 128
-ORDER = (0, 2, 3, 1)
+ORDER = (0, 2, 1, 3)
 
 
 def as_words(packed):
@@ -63,7 +63,7 @@ def tile_picked_sharedexp_relu_po_kernel(
         x_table = tile("x_table", [P, T], U32)
         x_table_scales = tile("x_table_scales", [P, T], U8)
         w1_raw = [tile("w1_raw%d" % i, [P, 2, H], F32) for i in range(2)]
-        w2_raw = [tile("w2_raw%d" % u, [P, PACK, HALF], F32) for u in range(2)]
+        w2_raw = [tile("w2_raw0", [P, PACK, HALF], F32), placed_tile("w2_raw1", [P, PACK, HALF], F32, 8192)]
         first, second, third, last = ORDER
         wt_sb = tile("wt_sb", [P, V], F32)
         w34_raw = tile("w34_raw", [P, 2 * H], I32)
@@ -77,6 +77,11 @@ def tile_picked_sharedexp_relu_po_kernel(
         for t in range(PACK):
             nc.vector.memset(z_rows[t][:], 0.0)
 
+        w2_bf = tile("w2_bf", [P, PACK, P, PACK], BF16)
+
+        z_all = tile("z_all", [P, PACK, S], F32)
+        nc.vector.memset(z_all[:, third, 0:1], 0.0)
+
         w1_by_rows = w1.rearrange("(p j) c -> p j c", j=PACK)
         w2_by_rows = w2.rearrange("(p j) c -> p j c", j=PACK)
         nc.sync.dma_start(w1_raw[0][:], w1_by_rows[:, :2])
@@ -85,9 +90,9 @@ def tile_picked_sharedexp_relu_po_kernel(
             nc.sync.dma_start(x_table_scales[r:P:32, :].bitcast(I32), x_scales[0, r:16:4, :].bitcast(I32))
         nc.sync.dma_start(w1_raw[1][:], w1_by_rows[:, 2:])
         nc.sync.dma_start(x_table[:].bitcast(I32), as_words(x_words))
+        nc.sync.dma_start(take_sb[:], take)
         nc.sync.dma_start(w34_raw_scales[:16, :].bitcast(I32), w3_scales[0].bitcast(I32))
         nc.sync.dma_start(w34_raw_scales[16:32, :].bitcast(I32), w4_scales[0].bitcast(I32))
-        nc.sync.dma_start(take_sb[:], take)
         for u in range(2):
             nc.sync.dma_start(w2_raw[u][:], w2_by_rows[:, :, u * HALF : (u + 1) * HALF])
         nc.sync.dma_start(wt_sb[:], wt.rearrange("(p j) v -> p j v", j=PACK)[:, 0, :])
@@ -116,34 +121,48 @@ def tile_picked_sharedexp_relu_po_kernel(
             quantize(w1_codes[:, u * HALF : (u + 1) * HALF], w1_scales[:, u * HALF : (u + 1) * HALF], w1_bf[:, u].rearrange("p v m j -> p (v m j)"))
 
         xg = [tile("xg%d" % h, [P, HALF], U32) for h in range(2)]
-        for h in range(2):
-            nc.vector.tensor_copy(xg[h][:], x_table[:].indirect(offs_sb[:, h * 16 : (h + 1) * 16]))
+        pieces = ((0, HALF), (HALF, CHUNK), (HALF + CHUNK, CHUNK))
+        for n0, count in pieces:
+            h, c0 = divmod(n0, HALF)
+            nc.vector.tensor_copy(xg[h][:, c0 : c0 + count], x_table[:].indirect(offs_sb[:, n0 // 16 : (n0 + count) // 16]))
 
         picked = {}
-        banks_used = 0
-        for k, t in enumerate(ORDER):
-            y_rows = sb.tile([P, S], F32, name="y_rows", tag="y_rows", bufs=2, align_bytes=64)
+
+        def hidden_rows(t, cuts, banks, bias):
+            y_rows = placed_tile("y_rows%d" % t, [P, S], F32, 12288 + 2048 * (ORDER.index(t) % 2))
             at = (2 * (t % 2) + t // 2) * P
-            pieces = [(0, HALF), (HALF, CHUNK), (HALF + CHUNK, CHUNK)] if k == 0 else [(0, HALF), (HALF, HALF)]
-            for n0, count in pieces:
-                acc = bank(banks_used % PACK, [P, count])
-                banks_used = banks_used + 1
-                h, c0 = divmod(n0, HALF)
-                mx_pass(acc[:], w1_codes[:, at : at + P], w1_scales[:, at : at + P], xg[h][:, c0 : c0 + count], xg_scales[:, n0 : n0 + count], True, True)
-                nc.scalar.activation(y_rows[:, n0 : n0 + count], acc[:], RELU)
-            if t == last:
-                picked[t] = placed_tile("picked_last", [P, V], F32, 0)
+            for (n0, count), b in zip(cuts, banks):
+                acc = bank(b, [P, count])
+                for m0 in range(n0, n0 + count, HALF):
+                    h, c0 = divmod(m0, HALF)
+                    width = min(count, HALF)
+                    mx_pass(
+                        acc[:, m0 - n0 : m0 - n0 + width], w1_codes[:, at : at + P], w1_scales[:, at : at + P],
+                        xg[h][:, c0 : c0 + width], xg_scales[:, m0 : m0 + width], True, True,
+                    )
+                nc.scalar.activation(y_rows[:, n0 : n0 + count], acc[:], RELU, bias=bias)
+            return y_rows
+
+        def pick(t, y_rows, parts):
+            if t in (third, last):
+                picked[t] = placed_tile("picked%d" % t, [P, V], F32, 8192 if t == third else 9216)
             else:
-                picked[t] = tile("picked%d" % (first if t == third else t), [P, V], F32)
-            nc.scalar.activation(picked[t][:], y_rows[:].indirect(take_sb[:]), COPY)
+                picked[t] = tile("picked%d" % t, [P, V], F32)
+            for v0 in range(0, V, V // parts):
+                nc.scalar.activation(picked[t][:, v0 : v0 + V // parts], y_rows[:].indirect(take_sb[:, v0 // 16 : (v0 + V // parts) // 16]), COPY)
+
+        halves = ((0, HALF), (HALF, HALF))
+        pick(first, hidden_rows(first, pieces, (0, 1, 2), 0.0), 2)
+        y_second = hidden_rows(second, ((0, S),), (2,), 0.0)
 
         def deal_packed(dealt, raw, run):
             nc.vector.tensor_copy(
                 dealt[:].rearrange("p t (c i) -> p c t i", i=run), raw[:].rearrange("p (c i t) -> p c t i", i=run, t=PACK)
             )
 
-        def scatter(t):
-            nc.vector.tensor_tensor(z_rows[t][:].indirect(take_sb[:]), picked[t][:], wt_sb[:], MULT)
+        def scatter(t, v0=0, count=V):
+            cols = slice(v0, v0 + count)
+            nc.vector.tensor_tensor(z_rows[t][:].indirect(take_sb[:, v0 // 16 : (v0 + count) // 16]), picked[t][:, cols], wt_sb[:, cols], MULT)
 
         w34_dealt_scales = tile("w34_dealt_scales", [P, PACK, P], U8)
         deal_packed(w34_dealt_scales, w34_raw_scales, 16)
@@ -151,8 +170,6 @@ def tile_picked_sharedexp_relu_po_kernel(
         for i in (1, 0):
             for q in range(4):
                 nc.sync.dma_start(w34_scales[32 * q + 4 * i : 32 * q + 4 * i + 4, :].bitcast(I32), dealt_rows[16 * i + 4 * q : 16 * i + 4 * q + 4, :])
-
-        w2_bf = tile("w2_bf", [P, PACK, P, PACK], BF16)
 
         def w2_views(u, ts):
             return (
@@ -162,11 +179,17 @@ def tile_picked_sharedexp_relu_po_kernel(
 
         nc.vector.tensor_copy(*w2_views(0, slice(0, 4)))
         nc.vector.tensor_scalar(*w2_views(1, slice(0, 4)), z_rows[first][:, 0:1], z_rows[second][:, 0:1], ADD, ADD)
+        pick(second, y_second, 1)
+        scatter(first, 0, V // 2)
         w2_codes = placed_tile("w2_codes", [P, H], U32, 4096)
         w2_scales = tile("w2_scales", [P, H], U8)
         quantize(w2_codes[:], w2_scales[:], w2_bf[:].rearrange("p t m j -> p (t m j)"))
-        scatter(first)
+        scatter(first, V // 2, V // 2)
+        nc.sync.dma_start(z_all[:, first, :], z_rows[first][:])
+        pick(third, hidden_rows(third, halves, (0, 3), 0.0), 1)
+        pick(last, hidden_rows(last, ((0, S),), (1,), 0.0), 1)
         scatter(second)
+        nc.sync.dma_start(z_all[:, second, :], z_rows[second][:])
         scatter(third)
 
         def deal_words(codes, i):
@@ -182,22 +205,19 @@ def tile_picked_sharedexp_relu_po_kernel(
             for t in range(PACK):
                 mx_pass(acc[:, t, :], w2_codes[:, t * P : (t + 1) * P], w2_scales[:, t * P : (t + 1) * P], xg[h][:, c0 : c0 + CHUNK], xg_scales[:, c * CHUNK : (c + 1) * CHUNK], True, True)
             nc.scalar.activation(
-                z2_bf[h][:, c0 : c0 + CHUNK, :], acc[:].rearrange("p t n -> p n t"), RELU, bias=z_rows[last][:, 0:1] if c == 3 else 0.0
+                z2_bf[h][:, c0 : c0 + CHUNK, :], acc[:].rearrange("p t n -> p n t"), RELU, bias=(0.0, z_rows[last][:, 0:1], 0.0, z_all[:, third, 0:1])[c]
             )
 
         w4_codes = placed_tile("w4_codes", [P, PACK, P], U32, 2048 + 64)
-        w3_codes = placed_tile("w3_codes", [P, PACK, P], U32, 0)
-        z_pairs = placed_tile("z_pairs", [P, 2, S, 2], BF16, 4096 + 64)
-        nc.vector.tensor_copy(z_pairs[:, first // 2, :, first % 2], z_rows[first][:])
+        w3_codes = placed_tile("w3_codes", [P, PACK, P], U32, 4096 + 64)
         deal_words(w4_codes, 1)
-        for t in (second, third):
-            nc.scalar.copy(z_pairs[:, t // 2, :, t % 2], z_rows[t][:])
+        nc.scalar.copy(z_all[:, third, :], z_rows[third][:])
         deal_words(w3_codes, 0)
 
         out_acc = [[bank(PACK * h + t, [P, HALF]) for t in range(PACK)] for h in range(2)]
 
         def shared_passes(h):
-            z2_codes = tile("z2_codes%d" % h, [P, HALF], U32)
+            z2_codes = placed_tile("z2_codes1", [P, HALF], U32, 9216) if h == 1 else tile("z2_codes0", [P, HALF], U32)
             z2_scales = tile("z2_scales%d" % h, [P, HALF], U8)
             quantize(z2_codes[:], z2_scales[:], z2_bf[h][:].rearrange("p n t -> p (n t)"))
             for t in range(PACK):
@@ -208,20 +228,29 @@ def tile_picked_sharedexp_relu_po_kernel(
         shared_passes(1)
 
         z_bf = [tile("z_bf%d" % h, [P, HALF, PACK], BF16) for h in range(2)]
-        for h in range(2):
-            nc.vector.tensor_copy(z_pairs[:, last // 2, h * HALF : (h + 1) * HALF, last % 2], z_rows[last][:, h * HALF : (h + 1) * HALF])
-        pair_words = z_pairs[:].rearrange("p u n e -> p (u n e)").bitcast(F32).rearrange("p (u n) -> p u n", u=2)
-        for h, copy in enumerate((nc.vector.tensor_copy, nc.vector.tensor_copy)):
+
+        def round_z(copy, n0, count):
+            h, c0 = divmod(n0, HALF)
             copy(
-                z_bf[h][:].rearrange("p n t -> p (n t)").bitcast(F32).rearrange("p (c i u) -> p c u i", i=4, u=2),
-                pair_words[:, :, h * HALF : (h + 1) * HALF].rearrange("p u (c i) -> p c u i", i=4),
+                z_bf[h][:, c0 : c0 + count, :].rearrange("p (c i) t -> p c t i", i=4),
+                z_all[:, :, n0 : n0 + count].rearrange("p t (c i) -> p c t i", i=4),
             )
-        for h in range(2):
+
+        def routed_passes(h):
             z_codes = tile("z_codes%d" % h, [P, HALF], U32)
             z_scales = tile("z_scales%d" % h, [P, HALF], U8)
             quantize(z_codes[:], z_scales[:], z_bf[h][:].rearrange("p n t -> p (n t)"))
             for t in range(PACK):
                 mx_pass(out_acc[h][t][:], w3_codes[:, t], w34_scales[:, t * P : (t + 1) * P], z_codes[:], z_scales[:], False, True)
+
+        for h in range(2):
+            nc.vector.tensor_copy(z_all[:, last, h * HALF : (h + 1) * HALF], z_rows[last][:, h * HALF : (h + 1) * HALF])
+        round_z(nc.scalar.copy, 0, 96)
+        round_z(nc.vector.tensor_copy, 96, 160)
+        round_z(nc.scalar.copy, HALF, 112)
+        round_z(nc.vector.tensor_copy, HALF + 112, 144)
+        routed_passes(0)
+        routed_passes(1)
 
         out_rows = out_0.rearrange("(p t) n -> p t n", t=PACK)
         out_words = as_words(out_1)

@@ -25,6 +25,7 @@ V = 256
 H = 512
 HALF = 256
 CHUNK = 128
+W2_CUT = 320
 ORDER = (0, 2, 1, 3)
 
 
@@ -63,7 +64,7 @@ def tile_picked_sharedexp_relu_po_kernel(
         x_table = tile("x_table", [P, T], U32)
         x_table_scales = tile("x_table_scales", [P, T], U8)
         w1_raw = [tile("w1_raw%d" % i, [P, 2, H], F32) for i in range(2)]
-        w2_raw = [tile("w2_raw0", [P, PACK, HALF], F32), placed_tile("w2_raw1", [P, PACK, HALF], F32, 8192)]
+        w2_raw = [tile("w2_raw0", [P, PACK, W2_CUT], F32), placed_tile("w2_raw1", [P, PACK, H - W2_CUT], F32, 8192)]
         first, second, third, last = ORDER
         wt_sb = tile("wt_sb", [P, V], F32)
         w34_raw = tile("w34_raw", [P, 2 * H], I32)
@@ -93,8 +94,8 @@ def tile_picked_sharedexp_relu_po_kernel(
         nc.sync.dma_start(take_sb[:], take)
         nc.sync.dma_start(w34_raw_scales[:16, :].bitcast(I32), w3_scales[0].bitcast(I32))
         nc.sync.dma_start(w34_raw_scales[16:32, :].bitcast(I32), w4_scales[0].bitcast(I32))
-        for u in range(2):
-            nc.sync.dma_start(w2_raw[u][:], w2_by_rows[:, :, u * HALF : (u + 1) * HALF])
+        nc.sync.dma_start(w2_raw[0][:], w2_by_rows[:, :, :W2_CUT])
+        nc.sync.dma_start(w2_raw[1][:], w2_by_rows[:, :, W2_CUT:])
         nc.sync.dma_start(wt_sb[:], wt.rearrange("(p j) v -> p j v", j=PACK)[:, 0, :])
         nc.sync.dma_start(w34_raw[:, H:], as_words(w4_words))
         nc.sync.dma_start(w34_raw[:, :H], as_words(w3_words))
@@ -173,7 +174,7 @@ def tile_picked_sharedexp_relu_po_kernel(
 
         def w2_views(u, ts):
             return (
-                w2_bf[:].rearrange("p t m j -> p m j t")[:, 64 * u : 64 * (u + 1), :, ts],
+                w2_bf[:].rearrange("p t m j -> p m j t")[:, slice(W2_CUT // PACK, P) if u else slice(0, W2_CUT // PACK), :, ts],
                 w2_raw[u][:].rearrange("p j (m t) -> p m j t", t=PACK)[:, :, :, ts],
             )
 
@@ -194,8 +195,8 @@ def tile_picked_sharedexp_relu_po_kernel(
 
         def deal_words(codes, i):
             nc.scalar.copy(
-                codes[:].rearrange("p t (c k) -> p c t k", k=4),
-                w34_raw[:, i * H : (i + 1) * H].bitcast(U32).rearrange("p (c k t) -> p c t k", k=4, t=PACK),
+                codes[:].rearrange("p t m -> p m t"),
+                w34_raw[:, i * H : (i + 1) * H].bitcast(U32).rearrange("p (m t) -> p m t", t=PACK),
             )
 
         z2_bf = [tile("z2_bf%d" % h, [P, HALF, PACK], BF16) for h in range(2)]

@@ -25,8 +25,6 @@ V = 256
 H = 512
 HALF = 256
 CHUNK = 128
-W2_CUT = 320
-ORDER = (0, 2, 1, 3)
 
 
 def as_words(packed):
@@ -39,14 +37,10 @@ def tile_picked_sharedexp_relu_po_kernel(
     nc = tc.nc
     with ExitStack() as ctx:
         sb = ctx.enter_context(tc.tile_pool(name="sb", bufs=1))
-        placed = ctx.enter_context(tc.tile_pool(name="placed", bufs=1))
         psum = ctx.enter_context(tc.psum_pool(name="psum", bufs=1))
 
         def tile(name, shape, dtype):
             return sb.tile(shape, dtype, name=name, align_bytes=64)
-
-        def placed_tile(name, shape, dtype, offset):
-            return placed.tile(shape, dtype, name=name, align_bytes=64, offset=offset)
 
         def bank(b, shape):
             return psum.tile(shape, F32, name="bank%d" % b, tag="bank%d" % b)
@@ -64,41 +58,43 @@ def tile_picked_sharedexp_relu_po_kernel(
         x_table = tile("x_table", [P, T], U32)
         x_table_scales = tile("x_table_scales", [P, T], U8)
         w1_raw = [tile("w1_raw%d" % i, [P, 2, H], F32) for i in range(2)]
-        w2_raw = [tile("w2_raw0", [P, PACK, W2_CUT], F32), placed_tile("w2_raw1", [P, PACK, H - W2_CUT], F32, 8192)]
-        first, second, third, last = ORDER
-        wt_sb = tile("wt_sb", [P, V], F32)
-        w34_raw = tile("w34_raw", [P, 2 * H], I32)
+        w2_raw = tile("w2_raw", [P, PACK, H], F32)
+        w3_raw = tile("w3_raw", [P, H], I32)
+        w4_raw = tile("w4_raw", [P, H], I32)
         w34_raw_scales = tile("w34_raw_scales", [P, H], U8)
+        w34_scales = tile("w34_scales", [P, H], U8)
         z_rows = [tile("z_rows%d" % t, [P, S], F32) for t in range(PACK)]
+        z_all = tile("z_all", [P, PACK, S], F32)
+        first, by_vector, second, third = 0, 2, 1, 3
+        wt_sb = tile("wt_sb", [P, V], F32)[:]
 
         nc.vector.memset(x_table_scales[:].bitcast(I32), 0)
         nc.vector.memset(w34_raw_scales[:].bitcast(I32), 0)
-        w34_scales = tile("w34_scales", [P, H], U8)
         nc.vector.memset(w34_scales[:].bitcast(I32), 0)
         for t in range(PACK):
             nc.vector.memset(z_rows[t][:], 0.0)
-
-        w2_bf = tile("w2_bf", [P, PACK, P, PACK], BF16)
-
-        z_all = tile("z_all", [P, PACK, S], F32)
-        nc.vector.memset(z_all[:, third, 0:1], 0.0)
+        nc.vector.memset(z_all[:, third, HALF - 1 : HALF + 1], 0.0)
+        nc.vector.memset(z_all[:, second, HALF : HALF + 1], 0.0)
+        picked = {t: tile("picked%d" % t, [P, V], F32) for t in (first, by_vector, second)}
+        zeros = [sb.tile([P, 1], F32, name="zero%d" % h, tag="z2_%d_scales" % h, align_bytes=64) for h in range(2)]
+        out_bias = sb.tile([P, 1], F32, name="out_bias", tag="out_scales", align_bytes=64)
+        for zero in zeros + [out_bias]:
+            nc.vector.memset(zero[:], 0.0)
 
         w1_by_rows = w1.rearrange("(p j) c -> p j c", j=PACK)
-        w2_by_rows = w2.rearrange("(p j) c -> p j c", j=PACK)
         nc.sync.dma_start(w1_raw[0][:], w1_by_rows[:, :2])
         nc.sync.dma_start(offs_sb[:], offs)
         for r in range(4):
             nc.sync.dma_start(x_table_scales[r:P:32, :].bitcast(I32), x_scales[0, r:16:4, :].bitcast(I32))
         nc.sync.dma_start(w1_raw[1][:], w1_by_rows[:, 2:])
         nc.sync.dma_start(x_table[:].bitcast(I32), as_words(x_words))
-        nc.sync.dma_start(take_sb[:], take)
+        nc.sync.dma_start(w4_raw[:], as_words(w4_words))
+        nc.sync.dma_start(w3_raw[:], as_words(w3_words))
         nc.sync.dma_start(w34_raw_scales[:16, :].bitcast(I32), w3_scales[0].bitcast(I32))
         nc.sync.dma_start(w34_raw_scales[16:32, :].bitcast(I32), w4_scales[0].bitcast(I32))
-        nc.sync.dma_start(w2_raw[0][:], w2_by_rows[:, :, :W2_CUT])
-        nc.sync.dma_start(w2_raw[1][:], w2_by_rows[:, :, W2_CUT:])
-        nc.sync.dma_start(wt_sb[:], wt.rearrange("(p j) v -> p j v", j=PACK)[:, 0, :])
-        nc.sync.dma_start(w34_raw[:, H:], as_words(w4_words))
-        nc.sync.dma_start(w34_raw[:, :H], as_words(w3_words))
+        nc.sync.dma_start(wt_sb, wt.rearrange("(p j) v -> p j v", j=PACK)[:, 0, :])
+        nc.sync.dma_start(take_sb[:], take)
+        nc.sync.dma_start(w2_raw[:], w2.rearrange("(p j) c -> p j c", j=PACK))
 
         w1_bf = tile("w1_bf", [P, 2, 2, P, PACK], BF16)
 
@@ -121,174 +117,177 @@ def tile_picked_sharedexp_relu_po_kernel(
         for u in range(2):
             quantize(w1_codes[:, u * HALF : (u + 1) * HALF], w1_scales[:, u * HALF : (u + 1) * HALF], w1_bf[:, u].rearrange("p v m j -> p (v m j)"))
 
-        xg = [tile("xg%d" % h, [P, HALF], U32) for h in range(2)]
-        pieces = ((0, HALF), (HALF, CHUNK), (HALF + CHUNK, CHUNK))
-        for n0, count in pieces:
-            h, c0 = divmod(n0, HALF)
-            nc.vector.tensor_copy(xg[h][:, c0 : c0 + count], x_table[:].indirect(offs_sb[:, n0 // 16 : (n0 + count) // 16]))
+        xg = tile("xg", [P, S], U32)
+        for h in range(2):
+            nc.vector.tensor_copy(xg[:, h * HALF : (h + 1) * HALF], x_table[:].indirect(offs_sb[:, h * HALF // 16 : (h + 1) * HALF // 16]))
 
-        picked = {}
+        y_rows = {}
 
-        def hidden_rows(t, cuts, banks, bias):
-            y_rows = placed_tile("y_rows%d" % t, [P, S], F32, 12288 + 2048 * (ORDER.index(t) % 2))
+        def y_passes(t, halves, b):
+            if t not in y_rows:
+                y_rows[t] = sb.tile([P, S], F32, name="y_rows%d" % t, tag="y_rows%d" % (first if t == third else t), align_bytes=64)
+            acc = bank(b, [P, len(halves) * HALF])
             at = (2 * (t % 2) + t // 2) * P
-            for (n0, count), b in zip(cuts, banks):
-                acc = bank(b, [P, count])
-                for m0 in range(n0, n0 + count, HALF):
-                    h, c0 = divmod(m0, HALF)
-                    width = min(count, HALF)
-                    mx_pass(
-                        acc[:, m0 - n0 : m0 - n0 + width], w1_codes[:, at : at + P], w1_scales[:, at : at + P],
-                        xg[h][:, c0 : c0 + width], xg_scales[:, m0 : m0 + width], True, True,
-                    )
-                nc.scalar.activation(y_rows[:, n0 : n0 + count], acc[:], RELU, bias=bias)
-            return y_rows
+            cols = slice(halves[0] * HALF, (halves[-1] + 1) * HALF)
+            mx_pass(acc[:], w1_codes[:, at : at + P], w1_scales[:, at : at + P], xg[:, cols], xg_scales[:, cols], True, True)
+            return y_rows[t][:, cols], acc[:]
 
-        def pick(t, y_rows, parts):
-            if t in (third, last):
-                picked[t] = placed_tile("picked%d" % t, [P, V], F32, 8192 if t == third else 9216)
-            else:
-                picked[t] = tile("picked%d" % t, [P, V], F32)
-            for v0 in range(0, V, V // parts):
-                nc.scalar.activation(picked[t][:, v0 : v0 + V // parts], y_rows[:].indirect(take_sb[:, v0 // 16 : (v0 + V // parts) // 16]), COPY)
+        def deal(dealt, raw, run):
+            nc.vector.tensor_copy(dealt.rearrange("p t (c i) -> p c t i", i=run), raw.rearrange("p (c i t) -> p c t i", i=run, t=PACK))
 
-        halves = ((0, HALF), (HALF, HALF))
-        pick(first, hidden_rows(first, pieces, (0, 1, 2), 0.0), 2)
-        y_second = hidden_rows(second, ((0, S),), (2,), 0.0)
+        def pick_weighted(t):
+            nc.vector.tensor_tensor(picked[t][:], y_rows[t][:].indirect(take_sb[:]), wt_sb, MULT)
 
-        def deal_packed(dealt, raw, run):
-            nc.vector.tensor_copy(
-                dealt[:].rearrange("p t (c i) -> p c t i", i=run), raw[:].rearrange("p (c i t) -> p c t i", i=run, t=PACK)
-            )
+        def scatter_on_scalar(t):
+            nc.scalar.activation(z_rows[t][:].indirect(take_sb[:]), picked[t][:], COPY)
 
-        def scatter(t, v0=0, count=V):
-            cols = slice(v0, v0 + count)
-            nc.vector.tensor_tensor(z_rows[t][:].indirect(take_sb[:, v0 // 16 : (v0 + count) // 16]), picked[t][:, cols], wt_sb[:, cols], MULT)
+        nc.scalar.activation(*y_passes(first, (0,), 0), RELU)
+        nc.scalar.activation(*y_passes(by_vector, (0,), 2), RELU)
 
+        w4_codes = tile("w4_codes", [P, PACK, P], I32)
+        w3_codes = tile("w3_codes", [P, PACK, P], I32)
+        deal(w4_codes[:], w4_raw[:], 4)
+        deal(w3_codes[:], w3_raw[:], 4)
         w34_dealt_scales = tile("w34_dealt_scales", [P, PACK, P], U8)
-        deal_packed(w34_dealt_scales, w34_raw_scales, 16)
+        deal(w34_dealt_scales[:], w34_raw_scales[:], 16)
         dealt_rows = w34_dealt_scales[:].rearrange("p t m -> p (t m)").bitcast(I32)
         for i in (1, 0):
             for q in range(4):
                 nc.sync.dma_start(w34_scales[32 * q + 4 * i : 32 * q + 4 * i + 4, :].bitcast(I32), dealt_rows[16 * i + 4 * q : 16 * i + 4 * q + 4, :])
 
-        def w2_views(u, ts):
-            return (
-                w2_bf[:].rearrange("p t m j -> p m j t")[:, slice(W2_CUT // PACK, P) if u else slice(0, W2_CUT // PACK), :, ts],
-                w2_raw[u][:].rearrange("p j (m t) -> p m j t", t=PACK)[:, :, :, ts],
-            )
-
-        nc.vector.tensor_copy(*w2_views(0, slice(0, 4)))
-        nc.vector.tensor_scalar(*w2_views(1, slice(0, 4)), z_rows[first][:, 0:1], z_rows[second][:, 0:1], ADD, ADD)
-        pick(second, y_second, 1)
-        scatter(first, 0, V // 2)
-        w2_codes = placed_tile("w2_codes", [P, H], U32, 4096)
-        w2_scales = tile("w2_scales", [P, H], U8)
-        quantize(w2_codes[:], w2_scales[:], w2_bf[:].rearrange("p t m j -> p (t m j)"))
-        scatter(first, V // 2, V // 2)
+        nc.scalar.activation(*y_passes(first, (1,), 1), RELU)
+        nc.scalar.activation(*y_passes(by_vector, (1,), 3), RELU)
+        nc.scalar.activation(*y_passes(second, (0, 1), 4), RELU)
+        pick_weighted(first)
+        nc.vector.tensor_copy(picked[by_vector][:], y_rows[by_vector][:].indirect(take_sb[:]))
+        scatter_on_scalar(first)
         nc.sync.dma_start(z_all[:, first, :], z_rows[first][:])
-        pick(third, hidden_rows(third, halves, (0, 3), 0.0), 1)
-        pick(last, hidden_rows(last, ((0, S),), (1,), 0.0), 1)
-        scatter(second)
-        nc.sync.dma_start(z_all[:, second, :], z_rows[second][:])
-        scatter(third)
+        pick_weighted(second)
+        nc.scalar.activation(*y_passes(third, (0, 1), 5), RELU)
+        scatter_on_scalar(second)
 
-        def deal_words(codes, i):
-            nc.scalar.copy(
-                codes[:].rearrange("p t m -> p m t"),
-                w34_raw[:, i * H : (i + 1) * H].bitcast(U32).rearrange("p (m t) -> p m t", t=PACK),
-            )
+        w2_codes = tile("w2_codes", [P, H], U32)
+        w2_scales = tile("w2_scales", [P, H], U8)
 
-        z2_bf = [tile("z2_bf%d" % h, [P, HALF, PACK], BF16) for h in range(2)]
-        for c in range(S // CHUNK):
-            acc = bank(PACK + c, [P, PACK, CHUNK])
-            h, c0 = divmod(c * CHUNK, HALF)
-            for t in range(PACK):
-                mx_pass(acc[:, t, :], w2_codes[:, t * P : (t + 1) * P], w2_scales[:, t * P : (t + 1) * P], xg[h][:, c0 : c0 + CHUNK], xg_scales[:, c * CHUNK : (c + 1) * CHUNK], True, True)
-            nc.scalar.activation(
-                z2_bf[h][:, c0 : c0 + CHUNK, :], acc[:].rearrange("p t n -> p n t"), RELU, bias=(0.0, z_rows[last][:, 0:1], 0.0, z_all[:, third, 0:1])[c]
-            )
-
-        w4_codes = placed_tile("w4_codes", [P, PACK, P], U32, 2048 + 64)
-        w3_codes = placed_tile("w3_codes", [P, PACK, P], U32, 4096 + 64)
-        deal_words(w4_codes, 1)
-        nc.scalar.copy(z_all[:, third, :], z_rows[third][:])
-        deal_words(w3_codes, 0)
-
-        out_acc = [[bank(PACK * h + t, [P, HALF]) for t in range(PACK)] for h in range(2)]
-
-        def shared_passes(h):
-            z2_codes = placed_tile("z2_codes1", [P, HALF], U32, 9216) if h == 1 else tile("z2_codes0", [P, HALF], U32)
-            z2_scales = tile("z2_scales%d" % h, [P, HALF], U8)
-            quantize(z2_codes[:], z2_scales[:], z2_bf[h][:].rearrange("p n t -> p (n t)"))
-            for t in range(PACK):
-                mx_pass(out_acc[h][t][:], w4_codes[:, t], w34_scales[4:P, t * P : (t + 1) * P], z2_codes[:], z2_scales[:], True, False)
-
-        shared_passes(0)
-        scatter(last)
-        shared_passes(1)
-
-        z_bf = [tile("z_bf%d" % h, [P, HALF, PACK], BF16) for h in range(2)]
-
-        def round_z(copy, n0, count):
-            h, c0 = divmod(n0, HALF)
-            copy(
-                z_bf[h][:, c0 : c0 + count, :].rearrange("p (c i) t -> p c t i", i=4),
-                z_all[:, :, n0 : n0 + count].rearrange("p t (c i) -> p c t i", i=4),
-            )
-
-        def routed_passes(h):
-            z_codes = tile("z_codes%d" % h, [P, HALF], U32)
-            z_scales = tile("z_scales%d" % h, [P, HALF], U8)
-            quantize(z_codes[:], z_scales[:], z_bf[h][:].rearrange("p n t -> p (n t)"))
-            for t in range(PACK):
-                mx_pass(out_acc[h][t][:], w3_codes[:, t], w34_scales[:, t * P : (t + 1) * P], z_codes[:], z_scales[:], False, True)
-
-        for h in range(2):
-            nc.vector.tensor_copy(z_all[:, last, h * HALF : (h + 1) * HALF], z_rows[last][:, h * HALF : (h + 1) * HALF])
-        round_z(nc.scalar.copy, 0, 96)
-        round_z(nc.vector.tensor_copy, 96, 160)
-        round_z(nc.scalar.copy, HALF, 112)
-        round_z(nc.vector.tensor_copy, HALF + 112, 144)
-        routed_passes(0)
-        routed_passes(1)
-
-        out_rows = out_0.rearrange("(p t) n -> p t n", t=PACK)
-        out_words = as_words(out_1)
-        out_scales = tile("out_scales", [P, S], U8)
-        out_f32 = tile("out_f32", [P, PACK, S], F32)
-        out_codes = tile("out_codes", [P, S], U32)
-
-        def round_out(copy, h, n0, count):
-            rounded = tile("out_bf%d_%d" % (h, n0), [P, count, PACK], BF16)
-            copy(
-                rounded[:].rearrange("p (c i) t -> p c t i", i=4),
-                out_f32[:, :, h * HALF + n0 : h * HALF + n0 + count].rearrange("p t (c i) -> p c t i", i=4),
+        def round_w2(u, tag, zero, other_zero):
+            rounded = sb.tile([P, 2, P, PACK], BF16, name="w2_bf%d" % u, tag=tag, align_bytes=64)
+            nc.vector.tensor_scalar(
+                rounded[:].rearrange("p t m j -> p m j t"), w2_raw[:].rearrange("p j (m t) -> p m j t", t=PACK)[:, :, :, 2 * u : 2 * u + 2],
+                zero, other_zero, ADD, ADD,
             )
             return rounded
 
-        def quantize_out(rounded, h, n0, count):
-            quantize(
-                out_codes[:, h * HALF + n0 : h * HALF + n0 + count],
-                out_scales[:, h * HALF + n0 : h * HALF + n0 + count],
-                rounded[:].rearrange("p n t -> p (n t)"),
-            )
+        def quantize_w2(u, rounded):
+            quantize(w2_codes[:, u * HALF : (u + 1) * HALF], w2_scales[:, u * HALF : (u + 1) * HALF], rounded[:].rearrange("p t m j -> p (t m j)"))
 
+        def scatter_on_vector(v0, v1):
+            nc.vector.tensor_tensor(z_rows[by_vector][:].indirect(take_sb[:, v0 // 16 : v1 // 16]), picked[by_vector][:, v0:v1], wt_sb[:, v0:v1], MULT)
+
+        w2_low = round_w2(0, "w2_bf0", 0.0, 0.0)
+        w2_high = round_w2(1, "w2_bf1", z_rows[by_vector][:, 0:1], z_all[:, second, HALF : HALF + 1])
+        quantize_w2(0, w2_low)
+        picked[third] = sb.tile([P, V], F32, name="picked%d" % third, tag="w2_raw", align_bytes=64)
+        pick_weighted(third)
+        scatter_on_scalar(third)
+        scatter_on_vector(0, V // 2)
+        quantize_w2(1, w2_high)
+        scatter_on_vector(V // 2, V)
+        nc.vector.tensor_scalar(
+            z_all[:, second, :], z_rows[second][:], z_all[:, third, HALF - 1 : HALF], z_all[:, third, HALF : HALF + 1], ADD, ADD
+        )
+        nc.vector.tensor_copy(z_all[:, by_vector, :], z_rows[by_vector][:])
         for h in range(2):
-            cols = slice(h * HALF, (h + 1) * HALF)
-            for t in range(PACK):
-                copy = nc.vector.tensor_copy if (h, t) in ((0, 1), (0, 3), (1, 1)) else nc.scalar.copy
-                copy(out_f32[:, t, cols], out_acc[h][t][:])
-                if h == 0 and t % 2 == 1:
-                    nc.sync.dma_start(out_rows[:, t - 1 : t + 1, cols], out_f32[:, t - 1 : t + 1, cols])
+            nc.vector.tensor_copy(z_all[:, third, h * HALF : (h + 1) * HALF], z_rows[third][:, h * HALF : (h + 1) * HALF])
+
+        z2_bf = [tile("z2_bf%d" % h, [P, HALF, PACK], BF16) for h in range(2)]
+        for c in range(S // CHUNK):
+            acc = bank((6, 7, 0, 6)[c], [P, PACK, CHUNK])
+            h, c0 = divmod(c * CHUNK, HALF)
+            for t in range(PACK) if c == 0 else reversed(range(PACK)):
+                mx_pass(acc[:, t, :], w2_codes[:, t * P : (t + 1) * P], w2_scales[:, t * P : (t + 1) * P], xg[:, c * CHUNK : (c + 1) * CHUNK], xg_scales[:, c * CHUNK : (c + 1) * CHUNK], True, True)
+            nc.scalar.activation(z2_bf[h][:, c0 : c0 + CHUNK, :], acc[:].rearrange("p t n -> p n t"), RELU)
+
+        def woven(rounded, rows):
+            return rounded.rearrange("p (c i) t -> p c t i", i=4), rows.rearrange("p t (c i) -> p c t i", i=4)
+
+        def interleave(rounded, rows):
+            nc.vector.tensor_copy(*woven(rounded, rows))
+
+        def quantized(name, grouped):
+            codes = tile(name + "_codes", [P, HALF], U32)
+            scales = tile(name + "_scales", [P, HALF], U8)
+            quantize(codes[:], scales[:], grouped[:].rearrange("p n t -> p (n t)"))
+            return codes, scales
+
+        pieces = (
+            ((range(0, 2), slice(0, HALF), 2), (range(2, 3), slice(0, HALF), 3), (range(3, 4), slice(0, HALF), 1)),
+            ((range(PACK), slice(0, CHUNK), 4), (range(PACK), slice(CHUNK, HALF), 5)),
+        )
+        out_acc = [[bank(b, [P, len(ts), cols.stop - cols.start]) for ts, cols, b in pieces[h]] for h in range(2)]
+
+        def out_passes(h, b, weights, weight_scales, codes, scales, opening):
+            ts, cols = pieces[h][b][:2]
+            for i, t in enumerate(ts):
+                mx_pass(
+                    out_acc[h][b][:, i, :], weights[:, t], weight_scales[:, t * P : (t + 1) * P], codes[:, cols], scales[:, cols],
+                    opening and i == 0, i == len(ts) - 1 and not opening,
+                )
+
+        def round_z(rounded, c, zero):
+            cols = slice(c % 2 * CHUNK, (c % 2 + 1) * CHUNK)
+            nc.vector.tensor_scalar_add(*woven(rounded[:, cols], z_all[:, :, c * CHUNK : (c + 1) * CHUNK]), zero)
+
+        z_bf = tile("z_bf0", [P, HALF, PACK], BF16)
+        round_z(z_bf, 0, zeros[0][:])
+        round_z(z_bf, 1, zeros[1][:])
+        shared = quantized("z2_0", z2_bf[0])
+        routed = quantized("z_0", z_bf)
+        for b in range(3):
+            out_passes(0, b, w4_codes, w34_scales[4:P], *shared, True)
+            out_passes(0, b, w3_codes, w34_scales[:], *routed, False)
+        z_bf = sb.tile([P, HALF, PACK], BF16, name="z_bf1", tag="z2_bf0", align_bytes=64)
+        round_z(z_bf, 2, 0.0)
+        shared = quantized("z2_1", z2_bf[1])
+        z_codes = tile("z_1_codes", [P, HALF], U32)
+        z_scales = tile("z_1_scales", [P, HALF], U8)
+        out_f32 = tile("out_f32", [P, PACK, S], F32)
+        for b in range(2):
+            cols = slice(b * CHUNK, (b + 1) * CHUNK)
+            if b == 1:
+                round_z(z_bf, 3, 0.0)
+                nc.vector.tensor_copy(out_f32[:, 3:, :HALF], out_acc[0][2][:])
+            quantize(z_codes[:, cols], z_scales[:, cols], z_bf[:, cols].rearrange("p n t -> p (n t)"))
+            out_passes(1, b, w4_codes, w34_scales[4:P], *shared, True)
+            out_passes(1, b, w3_codes, w34_scales[:], z_codes, z_scales, False)
+
+        out_rows = out_0.rearrange("(p t) n -> p t n", t=PACK)
+        out_scales = tile("out_scales", [P, S], U8)
+        out_codes = tile("out_codes", [P, S], U32)
+        nc.scalar.copy(out_f32[:, :2, :HALF], out_acc[0][0][:])
+        nc.sync.dma_start(out_rows[:, :2, :HALF], out_f32[:, :2, :HALF])
+        nc.scalar.copy(out_f32[:, 2:3, :HALF], out_acc[0][1][:])
+        nc.sync.dma_start(out_rows[:, 2:, :HALF], out_f32[:, 2:, :HALF])
+        for b in range(2):
+            nc.scalar.activation(out_f32[:, :, HALF + b * CHUNK : HALF + (b + 1) * CHUNK], out_acc[1][b][:], IDENTITY, bias=0.0 if b else out_bias[:])
         nc.sync.dma_start(out_rows[:, :, HALF:], out_f32[:, :, HALF:])
-        first_half = round_out(nc.vector.tensor_copy, 0, 0, HALF)
-        by_vector = round_out(nc.vector.tensor_copy, 1, 0, CHUNK)
-        by_scalar = round_out(nc.scalar.copy, 1, CHUNK, CHUNK)
-        quantize_out(first_half, 0, 0, HALF)
-        quantize_out(by_vector, 1, 0, CHUNK)
-        quantize_out(by_scalar, 1, CHUNK, CHUNK)
-        nc.sync.dma_start(out_words, out_codes[:].bitcast(I32))
+
+        out_bf = tile("out_bf", [P, S * PACK], BF16)
+
+        def rounded(n0, n1):
+            return out_bf[:, n0 * PACK : n1 * PACK].rearrange("p (n t) -> p n t", t=PACK)
+
+        def quantize_out(n0, n1):
+            quantize(out_codes[:, n0:n1], out_scales[:, n0:n1], out_bf[:, n0 * PACK : n1 * PACK])
+
+        interleave(rounded(0, HALF), out_f32[:, :, :HALF])
+        interleave(rounded(HALF, S - CHUNK), out_f32[:, :, HALF : S - CHUNK])
+        shared_from = S - CHUNK // 2
+        nc.scalar.copy(rounded(shared_from, S), out_acc[1][1][:, :, CHUNK // 2 :].rearrange("p t n -> p n t"))
+        quantize_out(0, HALF)
+        interleave(rounded(S - CHUNK, shared_from), out_f32[:, :, S - CHUNK : shared_from])
+        quantize_out(HALF, S - CHUNK)
+        quantize_out(S - CHUNK, S)
+        nc.sync.dma_start(as_words(out_1), out_codes[:].bitcast(I32))
         for r in range(4):
             queue = nc.sync if r < 2 else nc.scalar
             queue.dma_start(out_2[0, r:16:4, :].bitcast(I32), out_scales[r:P:32, :].bitcast(I32))

from contextlib import ExitStack

import concourse.mybir as mybir

FLOPS = 4 * 2 * 512 * 512 * 512

F32 = mybir.dt.float32
BF16 = mybir.dt.bfloat16
I32 = mybir.dt.int32
U32 = mybir.dt.uint32
U16 = mybir.dt.uint16
U8 = mybir.dt.uint8
FP8X4 = mybir.dt.float8_e4m3fn_x4
RELU = mybir.ActivationFunctionType.Relu
IDENTITY = mybir.ActivationFunctionType.Identity
COPY = mybir.ActivationFunctionType.Copy
MULT = mybir.AluOpType.mult
ADD = mybir.AluOpType.add

P = 128
PACK = 4
T = 2048
S = 512
V = 256
H = 512
HALF = 256
CHUNK = 128


def as_words(packed):
    return packed[0].rearrange("p n r -> p (n r)").bitcast(I32)


def tile_picked_sharedexp_relu_po_kernel(
    tc, x_words, x_scales, w1, wt, w2, w3_words, w3_scales, w4_words, w4_scales, offs, take, out_0, out_1, out_2
):
    nc = tc.nc
    with ExitStack() as ctx:
        sb = ctx.enter_context(tc.tile_pool(name="sb", bufs=1))
        psum = ctx.enter_context(tc.psum_pool(name="psum", bufs=1))

        def tile(name, shape, dtype):
            return sb.tile(shape, dtype, name=name, align_bytes=64)

        def bank(b, shape):
            return psum.tile(shape, F32, name="bank%d" % b, tag="bank%d" % b)

        def quantize(codes, scales, grouped):
            nc.vector.quantize_mx(out=codes.bitcast(FP8X4), scales=scales, in_=grouped)

        def mx_pass(acc, codes, scales, moving, moving_scales, start, stop):
            nc.tensor.matmul_mx(
                acc, lhsT=codes.bitcast(FP8X4), lhsT_scale=scales, rhs=moving.bitcast(FP8X4), rhs_scale=moving_scales, start=start, stop=stop
            )

        offs_sb = tile("offs_sb", [P, S // 16], U16)
        take_sb = tile("take_sb", [P, V // 16], U16)
        x_table = tile("x_table", [P, T], U32)
        x_table_scales = tile("x_table_scales", [P, T], U8)
        w1_raw = [tile("w1_raw%d" % i, [P, 2, H], F32) for i in range(2)]
        w2_raw = tile("w2_raw", [P, PACK, H], F32)
        w3_raw = tile("w3_raw", [P, H], I32)
        w4_raw = tile("w4_raw", [P, H], I32)
        w34_raw_scales = tile("w34_raw_scales", [P, H], U8)
        w34_scales = tile("w34_scales", [P, H], U8)
        z_rows = [tile("z_rows%d" % t, [P, S], F32) for t in range(PACK)]
        z_all = tile("z_all", [P, PACK, S], F32)
        first, by_vector, second, third = 0, 2, 1, 3
        wt_sb = tile("wt_sb", [P, V], F32)[:]

        nc.vector.memset(x_table_scales[:].bitcast(I32), 0)
        nc.vector.memset(w34_raw_scales[:].bitcast(I32), 0)
        nc.vector.memset(w34_scales[:].bitcast(I32), 0)
        for t in range(PACK):
            nc.vector.memset(z_rows[t][:], 0.0)
        nc.vector.memset(z_all[:, third, HALF - 1 : HALF + 1], 0.0)
        nc.vector.memset(z_all[:, second, HALF : HALF + 1], 0.0)
        picked = {t: tile("picked%d" % t, [P, V], F32) for t in (first, by_vector, second)}
        zeros = [sb.tile([P, 1], F32, name="zero%d" % h, tag="z2_%d_scales" % h, align_bytes=64) for h in range(2)]
        out_bias = sb.tile([P, 1], F32, name="out_bias", tag="out_scales", align_bytes=64)
        for zero in zeros + [out_bias]:
            nc.vector.memset(zero[:], 0.0)

        w1_by_rows = w1.rearrange("(p j) c -> p j c", j=PACK)
        nc.sync.dma_start(w1_raw[0][:], w1_by_rows[:, :2])
        nc.sync.dma_start(offs_sb[:], offs)
        for r in range(4):
            nc.sync.dma_start(x_table_scales[r:P:32, :].bitcast(I32), x_scales[0, r:16:4, :].bitcast(I32))
        nc.sync.dma_start(w1_raw[1][:], w1_by_rows[:, 2:])
        nc.sync.dma_start(x_table[:].bitcast(I32), as_words(x_words))
        nc.sync.dma_start(w4_raw[:], as_words(w4_words))
        nc.sync.dma_start(w3_raw[:], as_words(w3_words))
        nc.sync.dma_start(w34_raw_scales[:16, :].bitcast(I32), w3_scales[0].bitcast(I32))
        nc.sync.dma_start(w34_raw_scales[16:32, :].bitcast(I32), w4_scales[0].bitcast(I32))
        nc.sync.dma_start(wt_sb, wt.rearrange("(p j) v -> p j v", j=PACK)[:, 0, :])
        nc.sync.dma_start(take_sb[:], take)
        nc.sync.dma_start(w2_raw[:], w2.rearrange("(p j) c -> p j c", j=PACK))

        w1_bf = tile("w1_bf", [P, 2, 2, P, PACK], BF16)

        def w1_views(u, js):
            return (
                w1_bf[:, u].rearrange("p v m j -> p m j v")[:, :, js],
                w1_raw[js.start // 2][:].rearrange("p j (m v u) -> p u m j v", v=2, u=2)[:, u],
            )

        nc.scalar.copy(*w1_views(1, slice(0, 2)))
        nc.scalar.copy(*w1_views(1, slice(2, 4)))

        xg_scales = tile("xg_scales", [P, S], U8)
        nc.vector.tensor_copy(xg_scales[:], x_table_scales[:].indirect(offs_sb[:]))
        nc.vector.tensor_copy(*w1_views(0, slice(0, 2)))
        nc.vector.tensor_copy(*w1_views(0, slice(2, 4)))

        w1_codes = tile("w1_codes", [P, H], U32)
        w1_scales = tile("w1_scales", [P, H], U8)
        for u in range(2):
            quantize(w1_codes[:, u * HALF : (u + 1) * HALF], w1_scales[:, u * HALF : (u + 1) * HALF], w1_bf[:, u].rearrange("p v m j -> p (v m j)"))

        xg = tile("xg", [P, S], U32)
        for h in range(2):
            nc.vector.tensor_copy(xg[:, h * HALF : (h + 1) * HALF], x_table[:].indirect(offs_sb[:, h * HALF // 16 : (h + 1) * HALF // 16]))

        y_rows = {}

        def y_passes(t, halves, b):
            if t not in y_rows:
                y_rows[t] = sb.tile([P, S], F32, name="y_rows%d" % t, tag="y_rows%d" % (first if t == third else t), align_bytes=64)
            acc = bank(b, [P, len(halves) * HALF])
            at = (2 * (t % 2) + t // 2) * P
            cols = slice(halves[0] * HALF, (halves[-1] + 1) * HALF)
            mx_pass(acc[:], w1_codes[:, at : at + P], w1_scales[:, at : at + P], xg[:, cols], xg_scales[:, cols], True, True)
            return y_rows[t][:, cols], acc[:]

        def deal(dealt, raw, run):
            nc.vector.tensor_copy(dealt.rearrange("p t (c i) -> p c t i", i=run), raw.rearrange("p (c i t) -> p c t i", i=run, t=PACK))

        def pick_weighted(t):
            nc.vector.tensor_tensor(picked[t][:], y_rows[t][:].indirect(take_sb[:]), wt_sb, MULT)

        def scatter_on_scalar(t):
            nc.scalar.activation(z_rows[t][:].indirect(take_sb[:]), picked[t][:], COPY)

        nc.scalar.activation(*y_passes(first, (0,), 0), RELU)
        nc.scalar.activation(*y_passes(by_vector, (0,), 2), RELU)

        w4_codes = tile("w4_codes", [P, PACK, P], I32)
        w3_codes = tile("w3_codes", [P, PACK, P], I32)
        deal(w4_codes[:], w4_raw[:], 4)
        deal(w3_codes[:], w3_raw[:], 4)
        w34_dealt_scales = tile("w34_dealt_scales", [P, PACK, P], U8)
        deal(w34_dealt_scales[:], w34_raw_scales[:], 16)
        dealt_rows = w34_dealt_scales[:].rearrange("p t m -> p (t m)").bitcast(I32)
        for i in (1, 0):
            for q in range(4):
                nc.sync.dma_start(w34_scales[32 * q + 4 * i : 32 * q + 4 * i + 4, :].bitcast(I32), dealt_rows[16 * i + 4 * q : 16 * i + 4 * q + 4, :])

        nc.scalar.activation(*y_passes(first, (1,), 1), RELU)
        nc.scalar.activation(*y_passes(by_vector, (1,), 3), RELU)
        nc.scalar.activation(*y_passes(second, (0, 1), 4), RELU)
        pick_weighted(first)
        nc.vector.tensor_copy(picked[by_vector][:], y_rows[by_vector][:].indirect(take_sb[:]))
        scatter_on_scalar(first)
        nc.sync.dma_start(z_all[:, first, :], z_rows[first][:])
        pick_weighted(second)
        nc.scalar.activation(*y_passes(third, (0, 1), 5), RELU)
        scatter_on_scalar(second)

        w2_codes = tile("w2_codes", [P, H], U32)
        w2_scales = tile("w2_scales", [P, H], U8)

        def round_w2(u, tag, zero, other_zero):
            rounded = sb.tile([P, 2, P, PACK], BF16, name="w2_bf%d" % u, tag=tag, align_bytes=64)
            nc.vector.tensor_scalar(
                rounded[:].rearrange("p t m j -> p m j t"), w2_raw[:].rearrange("p j (m t) -> p m j t", t=PACK)[:, :, :, 2 * u : 2 * u + 2],
                zero, other_zero, ADD, ADD,
            )
            return rounded

        def quantize_w2(u, rounded):
            quantize(w2_codes[:, u * HALF : (u + 1) * HALF], w2_scales[:, u * HALF : (u + 1) * HALF], rounded[:].rearrange("p t m j -> p (t m j)"))

        def scatter_on_vector(v0, v1):
            nc.vector.tensor_tensor(z_rows[by_vector][:].indirect(take_sb[:, v0 // 16 : v1 // 16]), picked[by_vector][:, v0:v1], wt_sb[:, v0:v1], MULT)

        w2_low = round_w2(0, "w2_bf0", 0.0, 0.0)
        w2_high = round_w2(1, "w2_bf1", z_rows[by_vector][:, 0:1], z_all[:, second, HALF : HALF + 1])
        quantize_w2(0, w2_low)
        picked[third] = sb.tile([P, V], F32, name="picked%d" % third, tag="w2_raw", align_bytes=64)
        pick_weighted(third)
        scatter_on_scalar(third)
        scatter_on_vector(0, V // 2)
        quantize_w2(1, w2_high)
        scatter_on_vector(V // 2, V)
        nc.vector.tensor_scalar(
            z_all[:, second, :], z_rows[second][:], z_all[:, third, HALF - 1 : HALF], z_all[:, third, HALF : HALF + 1], ADD, ADD
        )
        nc.vector.tensor_copy(z_all[:, by_vector, :], z_rows[by_vector][:])
        for h in range(2):
            nc.vector.tensor_copy(z_all[:, third, h * HALF : (h + 1) * HALF], z_rows[third][:, h * HALF : (h + 1) * HALF])

        z2_bf = [tile("z2_bf%d" % h, [P, HALF, PACK], BF16) for h in range(2)]
        for c in range(S // CHUNK):
            acc = bank((6, 7, 0, 6)[c], [P, PACK, CHUNK])
            h, c0 = divmod(c * CHUNK, HALF)
            for t in range(PACK) if c == 0 else reversed(range(PACK)):
                mx_pass(acc[:, t, :], w2_codes[:, t * P : (t + 1) * P], w2_scales[:, t * P : (t + 1) * P], xg[:, c * CHUNK : (c + 1) * CHUNK], xg_scales[:, c * CHUNK : (c + 1) * CHUNK], True, True)
            nc.scalar.activation(z2_bf[h][:, c0 : c0 + CHUNK, :], acc[:].rearrange("p t n -> p n t"), RELU)

        def woven(rounded, rows):
            return rounded.rearrange("p (c i) t -> p c t i", i=4), rows.rearrange("p t (c i) -> p c t i", i=4)

        def interleave(rounded, rows):
            nc.vector.tensor_copy(*woven(rounded, rows))

        def quantized(name, grouped):
            codes = tile(name + "_codes", [P, HALF], U32)
            scales = tile(name + "_scales", [P, HALF], U8)
            quantize(codes[:], scales[:], grouped[:].rearrange("p n t -> p (n t)"))
            return codes, scales

        pieces = (
            ((range(0, 2), slice(0, HALF), 2), (range(2, 3), slice(0, HALF), 3), (range(3, 4), slice(0, HALF), 1)),
            ((range(PACK), slice(0, CHUNK), 4), (range(PACK), slice(CHUNK, HALF), 5)),
        )
        out_acc = [[bank(b, [P, len(ts), cols.stop - cols.start]) for ts, cols, b in pieces[h]] for h in range(2)]

        def out_passes(h, b, weights, weight_scales, codes, scales, opening):
            ts, cols = pieces[h][b][:2]
            for i, t in enumerate(ts):
                mx_pass(
                    out_acc[h][b][:, i, :], weights[:, t], weight_scales[:, t * P : (t + 1) * P], codes[:, cols], scales[:, cols],
                    opening and i == 0, i == len(ts) - 1 and not opening,
                )

        def round_z(rounded, c, zero):
            cols = slice(c % 2 * CHUNK, (c % 2 + 1) * CHUNK)
            nc.vector.tensor_scalar_add(*woven(rounded[:, cols], z_all[:, :, c * CHUNK : (c + 1) * CHUNK]), zero)

        z_bf = tile("z_bf0", [P, HALF, PACK], BF16)
        round_z(z_bf, 0, zeros[0][:])
        round_z(z_bf, 1, zeros[1][:])
        shared = quantized("z2_0", z2_bf[0])
        routed = quantized("z_0", z_bf)
        for b in range(3):
            out_passes(0, b, w4_codes, w34_scales[4:P], *shared, True)
            out_passes(0, b, w3_codes, w34_scales[:], *routed, False)
        z_bf = sb.tile([P, HALF, PACK], BF16, name="z_bf1", tag="z2_bf0", align_bytes=64)
        round_z(z_bf, 2, 0.0)
        shared = quantized("z2_1", z2_bf[1])
        z_codes = tile("z_1_codes", [P, HALF], U32)
        z_scales = tile("z_1_scales", [P, HALF], U8)
        out_f32 = tile("out_f32", [P, PACK, S], F32)
        for b in range(2):
            cols = slice(b * CHUNK, (b + 1) * CHUNK)
            if b == 1:
                round_z(z_bf, 3, 0.0)
                nc.vector.tensor_copy(out_f32[:, 3:, :HALF], out_acc[0][2][:])
            quantize(z_codes[:, cols], z_scales[:, cols], z_bf[:, cols].rearrange("p n t -> p (n t)"))
            out_passes(1, b, w4_codes, w34_scales[4:P], *shared, True)
            out_passes(1, b, w3_codes, w34_scales[:], z_codes, z_scales, False)

        out_rows = out_0.rearrange("(p t) n -> p t n", t=PACK)
        out_scales = tile("out_scales", [P, S], U8)
        out_codes = tile("out_codes", [P, S], U32)
        nc.scalar.copy(out_f32[:, :2, :HALF], out_acc[0][0][:])
        nc.sync.dma_start(out_rows[:, :2, :HALF], out_f32[:, :2, :HALF])
        nc.scalar.copy(out_f32[:, 2:3, :HALF], out_acc[0][1][:])
        nc.sync.dma_start(out_rows[:, 2:, :HALF], out_f32[:, 2:, :HALF])
        for b in range(2):
            nc.scalar.activation(out_f32[:, :, HALF + b * CHUNK : HALF + (b + 1) * CHUNK], out_acc[1][b][:], IDENTITY, bias=0.0 if b else out_bias[:])
        nc.sync.dma_start(out_rows[:, :, HALF:], out_f32[:, :, HALF:])

        out_bf = tile("out_bf", [P, S * PACK], BF16)

        def rounded(n0, n1):
            return out_bf[:, n0 * PACK : n1 * PACK].rearrange("p (n t) -> p n t", t=PACK)

        def quantize_out(n0, n1):
            quantize(out_codes[:, n0:n1], out_scales[:, n0:n1], out_bf[:, n0 * PACK : n1 * PACK])

        interleave(rounded(0, HALF), out_f32[:, :, :HALF])
        interleave(rounded(HALF, S - CHUNK), out_f32[:, :, HALF : S - CHUNK])
        shared_from = S - CHUNK // 2
        nc.scalar.copy(rounded(shared_from, S), out_acc[1][1][:, :, CHUNK // 2 :].rearrange("p t n -> p n t"))
        quantize_out(0, HALF)
        interleave(rounded(S - CHUNK, shared_from), out_f32[:, :, S - CHUNK : shared_from])
        quantize_out(HALF, S - CHUNK)
        quantize_out(S - CHUNK, S)
        nc.sync.dma_start(as_words(out_1), out_codes[:].bitcast(I32))
        for r in range(4):
            queue = nc.sync if r < 2 else nc.scalar
            queue.dma_start(out_2[0, r:16:4, :].bitcast(I32), out_scales[r:P:32, :].bitcast(I32))
